import numpy as np, ml_dtypes
CORES = [10,34,74,98]
N = 4
BF = ml_dtypes.bfloat16
V, G, W, CAP, QA, QB, RO = 1024, 768, 2560, 128, 4, 2, 4
def deal(rng, a):
    return np.stack([rng.permutation(np.resize(np.array(a), 8)) for q in range(N)])
def parts(rng):
    sh = (N, 8, 16, V)
    mid = rng.integers(20, 236, (N, 8, 16, 16)); kin = rng.integers(0, 16, (N, 8, 1, V))
    x = np.take_along_axis(mid, kin, 3) + rng.integers(-20, 21, sh)
    low = deal(rng, [0.003, 0.01, 0.03])[:, :, None, None]; flat = deal(rng, [0, 1])[:, :, None, None] == 1
    r = np.where(flat, 255, rng.integers(130, 256, sh)); r = np.where(rng.random(sh) < low, rng.integers(1, 130, sh), r)
    p = np.where(rng.random(sh) < 0.15, rng.integers(1, 130, sh), 0)
    keep = deal(rng, [0.4, 0.7, 0.9])[:, :, None, None]
    s = np.where(rng.random(sh) < keep, np.arange(V), rng.integers(0, W, sh))
    c = np.where(rng.random(sh) < 0.5, rng.integers(0, V, sh), rng.integers(0, W, sh))
    h = deal(rng, [180, 230, 500, 1000, 1200]) + rng.integers(0, 32, (N, 8))
    return x, r, p, c, s, h
def pack(x, r, p, c, s, h):
    v = {"x": x, "reach": r, "past": p}
    d = {k: np.ascontiguousarray(v[k].reshape(N, 128, V)).astype(np.float32).astype(BF) for k in v}
    d["cand"] = np.ascontiguousarray(c.reshape(N, 128, V)).astype(np.int32); d["succ"] = np.ascontiguousarray(s.reshape(N, 128, V)).astype(np.int32)
    d["th"] = h.reshape(N, 8, 1).astype(np.int32)
    return d
def setup_inputs(rng):
    return pack(*parts(rng))
def setup_inputs_ends(rng):
    sh = (N, 8, 16, V); one = (N, 8, 1, V)
    x = 255 * np.where(rng.random(one) < 0.7, rng.integers(0, 2, one), rng.integers(0, 2, sh))
    x = np.where((rng.random(one) < 0.2) & (rng.random(sh) < 0.3), x + np.where(x == 0, 1, -1), x)
    k = rng.random(one); r = np.where(k < 0.5, 255, np.where(k < 0.6, 1, np.where(rng.random(sh) < 0.5, 1, 255)))
    p = 255 * ((rng.random(one) < 0.25) & (rng.random(sh) < 0.2)).astype(np.int64)
    c = np.where(rng.random(sh) < 0.65, (W - 1) * rng.integers(0, 2, sh), rng.integers(0, W, sh))
    s = np.where((rng.random(one) < 0.5) | (rng.random(sh) < 0.65), (W - 1) * rng.integers(0, 2, sh), rng.integers(0, W, sh))
    h = 4095 * rng.integers(0, 2, (N, 8)); h[:, 0] = 0; h[:, 4] = 4095; h[:, 7] = 4095
    for a in (0, 1, V - QA, V - 1, G - 1): p[..., a] = 0; r[..., a] = 255
    p[..., 2] = 255; r[..., 2] = 1; x[..., 0] = 0; x[..., V - QA] = 0
    for a in (1, V - 1): x[:, 1::2, :, a] = 255; x[:, ::2, :, a] = 0
    c[..., 0] = 2; c[:, :, 15, 0] = V - 1
    c[..., V - QA] = 2; c[:, :, 14, V - QA] = V - 1; c[:, :, 15, V - QA] = 1
    s[..., 0] = 0; s[..., G - 1] = W - 1
    return pack(x, r, p, c, s, h)
def setup_inputs_corners(rng):
    x, r, p, c, s, h = parts(rng); act = np.arange(0, G, QB); here = np.arange(V); ptr = np.array([0, V - 1, V, V + G - 1, V + G, W - 1])
    for q in range(N):
        for g in range(8):
            k = (g + q) % 8
            if k < 6:
                n = (0, 1, CAP - 1, CAP, CAP + 1, len(act))[k]; a = rng.permutation(act)[:n]
                h[q, g] = 0; x[q, g] = x[q, g][:, rng.integers(0, 16, V)]; r[q, g] = 200; r[q, g, :, V - 1] = 5
                p[q, g] = np.where(rng.random((16, V)) < 0.05, 10, 0)
                w = np.tile(here, (16, 1)); w[rng.integers(0, 16, n), a] = V - 1; s[q, g] = w
            elif k == 6:
                h[q, g] = 4095; p[q, g] = 0; c[q, g] = here - here % QA + (here + QA - 1) % QA
            else:
                h[q, g] = 4095; full = rng.random(V) < 0.5; full[0] = True; full[V - 1] = False; m = rng.random(V) < 0.5; n = int(np.count_nonzero(m))
                w = p[q, g].copy(); w[:, full] = 255; p[q, g] = w
                w = np.where(rng.random((16, V)) < 0.5, rng.integers(V, W, (16, V)), (here + QA * rng.integers(0, V // QA, (16, V))) % V)
                w[:, m] = rng.choice(here[full], (16, n)); w[15, m] = rng.integers(0, V, n); c[q, g] = w
                s[q, g] = np.where(rng.random((16, V)) < 0.3, here, ptr[rng.integers(0, 6, (16, V))])
    return pack(x, r, p, c, s, h)
def setup_inputs_ties(rng):
    x, r, p, c, s, h = parts(rng); sh = (N, 8, 16, V)
    x = 8 * rng.integers(0, 2, sh); pool = rng.integers(0, V, (N, 8, 1, 24)); pool[..., 0] = 0; pool[..., 1] = V - 1; pool[..., 2] = V; pool[..., 3] = W - 1
    few = np.take_along_axis(pool, rng.integers(0, 24, sh), 3); c[:, ::2] = few[:, ::2]
    m = np.arange(16)[:, None] == rng.integers(0, 16, (N, 8, 1, 1))
    r = np.where(m, rng.integers(100, 102, sh), rng.integers(101, 256, sh)); p = np.where(m, rng.integers(99, 101, sh), 0)
    h = deal(rng, [24, 32, 40, 48, 64])
    return pack(x, r, p, c, s, h)
def setup_inputs_border(rng):
    x, r, p, c, s, h = parts(rng); x = rng.integers(0, 256, x.shape); h = rng.integers(1, 33, h.shape); s[...] = np.arange(V)
    goal = np.zeros((N, 8, 3), np.int64); e, y, w = G - 1, V - 3, V - 2
    for q in range(N):
        for g in range(8):
            n, turn = ((0, 0), (0, int(rng.integers(1, 3))), (CAP - 1, 0), (CAP, 0), (CAP + 1, 0), (G, 0))[(g + q) % 6]
            o = [4 * rng.permutation(G // 4 - 1) + i for i in range(4)]
            v = o[turn][0]; j = o[0][1]; v1 = o[1][1]; u = o[1][2]; b = o[3][1]; z = o[3][2]
            for a in (v, e, j, y, v1, w, u, b): s[q, g, :, a] = z; c[q, g, :, a] = rng.integers(V, W, 16)
            for a in (v, v1, u): r[q, g, :, a] = rng.integers(140, 200, 16); p[q, g, :, a] = rng.integers(0, 41, 16)
            for a in (e, j): r[q, g, :, a] = rng.integers(200, 255, 16); p[q, g, :, a] = 0
            for a in (y, w): r[q, g, :, a] = 255; p[q, g, :, a] = 0
            r[q, g, :, z] = 255; r[q, g, :, V - 1] = 1
            i, k = rng.integers(0, 16, 2); d = int(rng.integers(1, 41))
            r[q, g, :, b] = r[q, g, :, u]; p[q, g, :, b] = p[q, g, :, u]; r[q, g, i, b] -= d; p[q, g, k, b] += d
            for a, f in ((v, e), (j, y), (v1, y), (w, y), (u, b)): x[q, g, :, a] = x[q, g, :, f]
            for a, f in ((v, e), (j, y), (v1, j), (w, y), (u, b)): c[q, g, int(rng.integers(0, 16)), a] = f
            a = rng.permutation(np.setdiff1d(np.arange(0, G, QB), np.array([v, j])))[:n]
            s[q, g][rng.integers(0, 16, len(a)), a] = V - 1
            goal[q, g] = (e, u, j)
    k = np.arange(G, V - 3)
    for q in range(N):
        for g in range(8):
            see = np.concatenate([V + goal[(q + 1) % N, g], V + G + goal[(q - 1) % N, g]])
            r[q, g, :, G:V - 3] = 255; p[q, g, :, G:V - 3] = 0
            s[q, g][rng.integers(0, 16, len(k)), k] = see[((k - G) // 4) % 6]
    return pack(x, r, p, c, s, h)
def setup_inputs_spread(rng):
    sh = (N, 8, 16, V); one = (N, 8, 1, V)
    def uneven(): return np.floor(np.exp2(8 * rng.random(one)) * rng.random(sh)).astype(np.int64)
    def lean():
        e = deal(rng, [1.0, 2.0, 4.0])[:, :, None, None]; v = np.minimum((W * rng.random(sh) ** e).astype(np.int64), W - 1)
        return np.where(deal(rng, [0, 0, 1])[:, :, None, None] == 1, W - 1 - v, v)
    x = uneven(); r = np.maximum(255 - uneven(), 1); p = np.where(rng.random(one) < 0.3, uneven(), 0)
    c = lean(); s = np.where(rng.random(one) < rng.random(sh), np.arange(V), lean())
    h = np.minimum(np.floor(np.exp2(12 * rng.random((N, 8)))).astype(np.int64), 4095)
    return pack(x, r, p, c, s, h)
def check_inputs(d):
    bad = []
    for k, lo, hi in (("x", 0, 255), ("reach", 1, 255), ("past", 0, 255), ("cand", 0, W - 1), ("succ", 0, W - 1), ("th", 0, 4095)):
        a = np.asarray(d[k]).astype(np.float64)
        if not (np.all(a >= lo) and np.all(a <= hi)): bad.append("range of " + k)
        elif not np.all(a == np.floor(a)): bad.append("whole numbers in " + k)
    return bad
def at(a, ix):
    return np.take_along_axis(a, ix[:, :, None, :], 3)
def reference(x, reach, past, cand, succ, th):
    X = x.astype(np.float32).astype(np.int32).reshape(N, 8, 16, V)
    R = reach.astype(np.float32).astype(np.int32).reshape(N, 8, 16, V); P = past.astype(np.float32).astype(np.int32).reshape(N, 8, 16, V)
    R = np.concatenate([R, np.roll(R[..., :G], -1, axis=0), np.roll(R[..., :G], 1, axis=0)], axis=3)
    P = np.concatenate([P, np.roll(P[..., :G], -1, axis=0), np.roll(P[..., :G], 1, axis=0)], axis=3)
    C = cand.astype(np.int64).reshape(N, 8, 16, V); S = succ.astype(np.int64).reshape(N, 8, 16, V); H = th.astype(np.int64).reshape(N, 8)
    F = np.zeros((N, 8, W), np.int64) + np.arange(W); M = np.zeros(N, np.int64); odd = (np.arange(16) % 2 == 1)[:, None]; NONE = 2 ** 20
    qi, gi = np.arange(N)[:, None, None], np.arange(8)[None, :, None]
    for t in range(RO):
        r_old, p_old, f_old = R[..., :G].copy(), P[..., :G].copy(), F[..., :G].copy()
        a = slice(t % QA, V, QA); v = np.arange(t % QA, V, QA); L = len(v)
        c = np.take_along_axis(F, C[..., a].reshape(N, 8, 16 * L), 2)
        xc, rc, pc = [at(w, i).reshape(N, 8, 16, 16, L) for w, i in ((X, np.minimum(c, V - 1)), (R, c), (P, c))]
        xv, rv, pv = [w[..., a][:, :, :, None, :] for w in (X, R, P)]
        c = c.reshape(N, 8, 16, L); ordered = np.any((rv <= pc) | (rc <= pv), axis=2)
        fit = ~ordered & (c < V) & (c % QA != t % QA)
        D = np.where(fit, np.add.reduce(np.abs(xc - xv), axis=2), NONE)
        k = np.argmin(D, axis=2)[:, :, None, :]
        b = np.take_along_axis(c, k, 2)[:, :, 0]; D = np.take_along_axis(D, k, 2)[:, :, 0].astype(np.int64); has = D < NONE; b = np.where(has, b, 0)
        C[..., a] = np.where(ordered & has[:, :, None, :], at(C, b), C[..., a])
        asks = has & (D < H[:, :, None] + (M & 31)[:, None, None]); key = np.where(asks, D * V + v, 2 ** 40)
        best = np.full((N, 8, V), 2 ** 40, np.int64); np.minimum.at(best, (qi, gi, b), key)
        win = asks & (np.take_along_axis(best, b, 2) == key); m = win[:, :, None, :]
        xb, rb, pb, sb = at(X, b), at(R, b), at(P, b), at(S, b)
        X[..., a] = np.where(m, (X[..., a] + xb) >> 1, X[..., a])
        R[..., a] = np.where(m, np.minimum(R[..., a], rb), R[..., a]); P[..., a] = np.where(m, np.maximum(P[..., a], pb), P[..., a])
        S[..., a] = np.where(m & odd, sb, S[..., a])
        i, j, l = np.nonzero(win); F[i, j, b[i, j, l]] = v[l]
        M = np.add.reduce(win.astype(np.int64).reshape(N, -1), axis=1)
        a = slice(t % QB, V, QB); L = len(range(t % QB, V, QB))
        c = np.take_along_axis(F, S[..., a].reshape(N, 8, 16 * L), 2)
        low = np.min(at(R, c).reshape(N, 8, 16, 16, L), axis=3); R[..., a] = np.minimum(R[..., a], low)
        ch = np.any(R[..., :G] != r_old, axis=2) | np.any(P[..., :G] != p_old, axis=2) | (F[..., :G] != f_old)
        go = ch & (np.add.accumulate(ch.astype(np.int64), axis=2) <= CAP)
        for turn, o in ((-1, V), (1, V + G)):
            w = np.roll(go, turn, axis=0); m = w[:, :, None, :]; f = np.roll(F[..., :G], turn, axis=0)
            R[..., o:o + G] = np.where(m, np.roll(R[..., :G], turn, axis=0), R[..., o:o + G])
            P[..., o:o + G] = np.where(m, np.roll(P[..., :G], turn, axis=0), P[..., o:o + G])
            F[..., o:o + G] = np.where(w & (f < G), f + o, F[..., o:o + G])
    return {"yx": X.reshape(N, 128, V).astype(np.float32).astype(BF), "yr": np.ascontiguousarray(R[..., :V]).reshape(N, 128, V).astype(np.float32).astype(BF), "yc": C.reshape(N, 128, V).astype(np.float32)}

@@ -1,0 +1,610 @@
+import math
+from concourse.bass import DstId, RemoteDMATransfer
+from concourse.mybir import AluOpType as ALU, AxisListType, ActivationFunctionType as AF
+
+V, G, W, N, ROUNDS = 1024, 768, 2560, 4, 4
+BIGX = 8192.0
+HASLIM = 4100.0 * 1024
+EQ = 1048576.0
+NS_P = (2, 3, 4, 5, 6, 7)
+NX_S = (6, 7)
+NV3 = 1
+
+b, f, i4, u2 = "bfloat16", "float32", "int32", "uint16"
+_S = {
+    "X": (1024, b), "R": (1024, b), "P": (1024, b), "xF": (2560, b), "RF": (2560, b), "PF": (2560, b), "xm": (1024, b),
+    "FB": (1280, b), "IB": (1024, b), "ni": (256, i4),
+    "ci": (1024, i4), "si": (1024, i4), "CF": (1024, f), "CfE": (1024, f), "CfO": (1024, f), "NHI": (256, b), "NLO": (256, b),
+    "SO": (1024, f), "SE": (1024, f), "SL0": (512, u2), "SL1": (512, u2),
+    "D1": (512, f), "T1": (512, f), "T2": (496, f), "ckf": (256, f), "CK0": (256, u2), "CK1": (256, u2), "CK2": (256, u2), "CK3": (256, u2),
+    "ones": (512, b), "I": (128, b), "nI": (128, b), "bI": (128, b), "U": (128, b), "E0": (128, b), "B16": (128, b),
+    "EK": (2048, b), "BL": (2048, b), "SelL": (2048, b), "RH": (2048, b), "kc": (512, b), "rst": (1024, b),
+    "SA": (128, b), "SB": (128, b), "SN": (128, b), "rows2": (256, b), "zb": (128, b),
+    "selD": (16, b), "selO": (16, b), "selp": (16, b), "seln": (16, b), "sFp": (16, b), "sFn": (16, b), "FS": (16, b), "FH": (16, b), "gm": (16, f),
+    "gmi": (16, i4), "mi16": (16, f), "mp": (16, f), "pw": (16, f), "sj": (16, f),
+    "pi": (1, i4), "gi": (1, i4), "ii": (1, i4), "ei": (1, i4), "oki": (1, i4), "mI": (128, i4), "mG": (128, i4), "mGf": (128, f),
+    "pf": (1, f), "gf": (1, f), "iF": (1, f), "i4c": (1, f), "modd": (1, f), "meven": (1, f), "okc": (1, f), "ekc": (1, f),
+    "wcol": (1, f), "il1": (1, f), "wlo": (1, f), "whi": (1, f), "wF": (1, f), "wFn": (1, f), "fhc": (1, f), "c7": (1, f), "c8": (1, f),
+    "cb": (2, f), "VL": (128, f), "VR": (96, f), "CC": (96, f), "V0": (96, f), "NG": (96, f), "NG1": (96, f),
+    "thr": (8, i4), "thb": (8, i4), "thK": (16, f), "thC": (16, f), "Mf": (1, f), "Mi": (1, i4), "Mj": (1, i4), "Mk": (1, f),
+    "xv2": (512, b), "Rv2": (512, b), "Pv2": (512, b), "dx": (4096, b), "ab": (4096, b), "oR": (4096, b), "oP": (4096, b), "pc": (4096, b),
+    "ka": (256, f), "t1": (256, f), "wk": (512, f), "wi": (128, i4), "dec": (32, b), "dec2": (48, b), "rowsN": (256, b), "nl": (16, u2),
+    "bits": (256, b), "Ae": (256, b), "Ao": (256, b), "Bk": (256, b), "tr": (512, b), "mx": (16, f), "win": (16, b), "rowsW": (512, b),
+    "bd": (32, f), "bl": (16, f), "bq": (32, f), "bq2": (32, f), "LL": (32, u2), "bu": (16, u2), "Rn": (256, b), "Pn": (256, b), "xs": (256, f), "xi": (256, i4),
+    "sn": (256, f), "FL": (64, u2), "g3": (8192, b), "s3": (8192, b), "oi": (256, f), "dC": (256, f),
+    "ch": (96, b), "xw": (768, f), "pos": (96, b), "FpT": (96, f), "dF": (96, f), "Fpb": (96, b), "rowsP": (768, b), "rowsF": (768, b), "pl": (48, u2), "SLB": (896, b),
+    "GRa": (896, b), "GRb": (896, b), "GPa": (896, b), "GPb": (896, b),
+}
+_WHERE, _POOL = {}, {f: 0, i4: 0, u2: 0, b: 0}
+SCRATCH = {}
+_OWN = ("nl", "pl", "FL", "LL", "bu", "SelL", "SA", "SB", "SN")
+for _n, (_c, _d) in _S.items():
+    if _c <= 128 and _n not in _OWN:
+        _WHERE[_n] = ("pool_" + _d, _POOL[_d]); _POOL[_d] += _c + (-_c) % 16
+    else:
+        SCRATCH[_n] = ("sbuf", [128, _c], _d); _WHERE[_n] = (_n, 0)
+for _d in _POOL:
+    if _POOL[_d]:
+        SCRATCH["pool_" + _d] = ("sbuf", [128, _POOL[_d]], _d)
+for _r in range(3):
+    for _n, _c, _d in (("SRP%d", 256, b), ("SLL%d", 56, u2), ("LRa%d", 256, b), ("LRb%d", 256, b), ("LLa%d", 56, u2), ("LLb%d", 56, u2)):
+        SCRATCH[_n % _r] = ("sbuf", [128, _c], _d); _WHERE[_n % _r] = (_n % _r, 0)
+for _r in range(8):
+    SCRATCH["pb%d" % _r] = ("psum", [128, 512], f); _WHERE["pb%d" % _r] = ("pb%d" % _r, 0)
+ND = 24
+SEMAPHORES = ["qv", "qs", "qt", "qg", "iR", "iP", "loc", "li"] + ["aR%d" % r for r in range(3)] + ["aL%d" % r for r in range(3)] + ["d%d" % k for k in range(ND)]
+
+
+def rank_program(g, core, T, topo):
+    rank = T.rank_of(core)
+    if rank is None:
+        return
+    eng = {"v": g.vector, "s": g.scalar, "t": g.tensor, "g": g, "y": g.sync}
+    cnt = {q: 0 for q in eng}; clk = {q: {} for q in eng}; hist = {}; info = []; total = {}; nd = [0]
+
+    def A(n, c0=0, c1=None, st=1, p0=0, p1=128):
+        t, o = _WHERE[n]
+        if c1 is None:
+            c1 = _S[n][0] if n in _S else SCRATCH[n][1][1]
+        ap = T[t][p0:p1, o + c0:o + c1] if st == 1 else T[t][p0:p1, o + c0:o + c1:st]
+        return (ap, [(n, c0, c1, st)])
+
+    def IND(w, o):
+        return (w[0].indirect(o[0]), w[1] + o[1])
+
+    def HB(ap):
+        return (ap, [])
+
+    def covers(a0, a1, st, e):
+        return a0 <= e[0] and e[1] <= a1 and (st == 1 or (e[4] == st and (e[0] - a0) % st == 0))
+
+    def sync(q, rd, wr, me):
+        need = set()
+        for regs, isw in ((rd, False), (wr, True)):
+            for n, a0, a1, st in regs:
+                ps = n[:2] == "pb"
+                for e in hist.get(n, ()):
+                    over = e[0] < a1 and a0 < e[1] and (e[0] - a0) % math.gcd(st, e[4]) == 0
+                    eq = info[e[2]][0]
+                    if ps:
+                        if eq != q or (over and e[3] and q != "t"):
+                            need.add(e[2])
+                    elif over and (e[3] or isw):
+                        need.add(e[2])
+        for o in sorted(need, reverse=True):
+            _, sem, val, ck = info[o]
+            if clk[q].get(sem, 0) >= val:
+                continue
+            eng[q].wait_ge(T.sem[sem], val)
+            for s, v in list(ck.items()) + [(sem, val)]:
+                if clk[q].get(s, 0) < v:
+                    clk[q][s] = v
+        for regs, isw in ((rd, False), (wr, True)):
+            for n, a0, a1, st in regs:
+                ps = n[:2] == "pb"
+                if ps:
+                    h = [e for e in hist.get(n, ()) if info[e[2]][0] == me[1] and not (covers(a0, a1, st, e) and isw == e[3])]
+                elif isw:
+                    h = [e for e in hist.get(n, ()) if not covers(a0, a1, st, e)]
+                else:
+                    h = [e for e in hist.get(n, ()) if not (not e[3] and covers(a0, a1, st, e) and info[e[2]][0] == q)]
+                h.append((a0, a1, me[0], isw, st)); hist[n] = h
+
+    def op(q, call, rd, wr):
+        me = len(info)
+        rr = [x for r in rd for x in r[1]]; ww = [x for r in wr for x in r[1]]
+        info.append((q, "q" + q, cnt[q] + 1, {}))
+        sync(q, rr, ww, (me, q))
+        if q == "g" and clk[q].get("qg", 0) < cnt[q]:
+            g.wait_ge(T.sem["qg"], cnt[q]); clk[q]["qg"] = cnt[q]
+        cnt[q] += 1
+        info[me] = (q, "q" + q, cnt[q], dict(clk[q]))
+        call(eng[q]).then_inc(T.sem["q" + q], 1); total["q" + q] = cnt[q]
+
+    def dma(q, out, in_):
+        me = len(info); s = "d%d" % nd[0]; nd[0] += 1
+        info.append(("d" + s, s, 16, {}))
+        sync(q, in_[1], out[1], (me, "d" + s))
+        info[me] = ("d" + s, s, 16, dict(clk[q])); total[s] = 16
+        eng[q].dma_start(out=out[0], in_=in_[0]).then_inc(T.sem[s], 16)
+
+    def arrive(sem, val, regs):
+        me = len(info); info.append(("x", sem, val, {})); total[sem] = val
+        for r in regs:
+            for n, a0, a1, st in r[1]:
+                hist.setdefault(n, []).append((a0, a1, me, True, st))
+
+    prev, nxt = T.cores[(rank - 1) % N], T.cores[(rank + 1) % N]
+    mk = min(topo.mask(core, prev), topo.mask(core, nxt))
+    ne = len([e for e in topo.engines(core, prev) if mk >> e & 1])
+
+    def send(src, to_prev, to_next, sem, loc="loc"):
+        sync("g", src[1], [], (len(info), "x")); info.append(("x", loc, 2 * ne, {}))
+        ids = []
+        for d in (prev, nxt):
+            rid, pid, _ = topo.addr(d); ids.append(DstId(rid=rid, pnc=pid))
+        g.remote_dma_fused([RemoteDMATransfer(dst_ids=ids, dma_engine_mask=mk, remote_sem=T.sem[sem], srcs=[src[0]], dsts=[to_prev[0], to_next[0]])], local_sem=T.sem[loc])
+        total[loc] = total.get(loc, 0) + ne
+
+    def cp(q, out, in_):
+        if q == "s":
+            op("s", lambda e: e.activation(out=out[0], in_=in_[0], func=AF.Copy), [in_], [out])
+        else:
+            op("v", lambda e: e.tensor_copy(out=out[0], in_=in_[0]), [in_], [out])
+
+    def tt(out, a, c, o):
+        op("v", lambda e: e.tensor_tensor(out=out[0], in0=a[0], in1=c[0], op=o), [a, c], [out])
+
+    def ts(out, a, s1, o1, s2=None, o2=None):
+        rd = [a] + [s for s in (s1, s2) if isinstance(s, tuple)]
+        v1 = s1[0] if isinstance(s1, tuple) else s1
+        v2 = s2[0] if isinstance(s2, tuple) else s2
+        if o2 is None:
+            op("v", lambda e: e.tensor_scalar(out=out[0], in0=a[0], scalar1=v1, scalar2=None, op0=o1), rd, [out])
+        else:
+            op("v", lambda e: e.tensor_scalar(out=out[0], in0=a[0], scalar1=v1, scalar2=v2, op0=o1, op1=o2), rd, [out])
+
+    def act(out, in_, fn, bias=None, scale=None, accum=None):
+        kw = {}
+        rd = [in_]; wr = [out]
+        if bias is not None:
+            kw["bias"] = bias[0]; rd.append(bias)
+        if scale is not None:
+            kw["scale"] = scale[0]; rd.append(scale)
+        if accum is not None:
+            kw["accum_out"] = accum[0]; wr.append(accum)
+        op("s", lambda e: e.activation(out=out[0], in_=in_[0], func=fn, **kw), rd, wr)
+
+    def ms(out, c):
+        op("v", lambda e: e.memset(out[0], c), [], [out])
+
+    def mm(out, l, r, start, stop):
+        op("t", lambda e: e.matmul(out=out[0], lhsT=l[0], rhs=r[0], start=start, stop=stop), [l, r], [out])
+
+    def iota(out, pat, base, cmul, small=False):
+        kw = {"allow_small_or_imprecise_dtypes": True} if small else {}
+        op("g", lambda e: e.iota(out[0], pat, base, cmul, **kw), [], [out])
+
+    def sel(out, in_, pat, o, fill, base, cmul):
+        op("g", lambda e: e.affine_select(out[0], in_[0], pat, o, fill, base, cmul), [in_], [out])
+
+    def rsum(out, in_):
+        op("v", lambda e: e.tensor_reduce(out=out[0], in_=in_[0], axis=AxisListType.X, op=ALU.add), [in_], [out])
+
+    def dup(q, out, src, t):
+        for h in (0, 256):
+            cp(q, A(out, h, h + 256), A(src, t, V, 4))
+
+    def cklist_d(t):
+        for e, src in ((0, "CfE"), (1, "CfO")):
+            for i in range(16):
+                sel(A("D1", 16 * e + i, 512, 32), A(src, 4 * i + t, V, 64), [[0, 16]], ALU.is_equal, 0.0, 0, 0)
+
+    def turn():
+        op("v", lambda e: e.transpose(out=A("T1")[0], in_=A("D1")[0]), [A("D1")], [A("T1")])
+
+    def cklist_t():
+        turn()
+        tt(A("T2"), A("T1", 0, 496), A("T1", 16, 512), ALU.add)
+        for k in range(16):
+            sel(A("ckf", 16 * k, 16 * k + 16), A("T2", k, 496, 32), [[0, 16]], ALU.is_equal, 0.0, 0, 0)
+
+    def halves(t, which):
+        n, o, s = (("NHI", ALU.arith_shift_right, 6), ("NLO", ALU.bitwise_and, 63))[which]
+        ts(A("ni"), A("ci", t, V, 4), s, o); cp("v", A(n), A("ni"))
+
+    def xgather(t, kk):
+        s = (512 * kk, 512 * kk + 512)
+        tt(A("dx", *s), IND(A("xF"), A("CK%d" % t, 32 * kk, 32 * kk + 32)), A("xv2"), ALU.subtract)
+
+    def xabs(kk):
+        s = (512 * kk, 512 * kk + 512)
+        act(A("ab", *s), A("dx", *s), AF.Abs)
+
+    def keyinit():
+        for half in (0, 1):
+            o = A("pb%d" % half, 0, 256)
+            mm(o, A("E0"), A("kc", 256 * half, 256 * half + 256), True, False)
+            for hv in range(4):
+                h, var = hv // 2, hv % 2
+                mm(o, A(("NHI", "NLO")[var], 128 * h, 128 * h + 128), A("RH", 512 * hv + 256 * half, 512 * hv + 256 * half + 256), False, False)
+
+    def keymm(kk, buf, w, last=False):
+        bank = "pb%d" % (kk // 4)
+        for k in (2 * kk, 2 * kk + 1):
+            for h in (0, 1):
+                o = 32 * (k % 8) + h
+                mm(A(bank, o, o + 32 - h, 2), A(buf, 256 * k + 128 * h, 256 * k + 128 * h + 128), A(w), False, last and k % 8 == 7 and h == 1)
+
+    def bits2list(out, src, n):
+        for i in range(16):
+            mm(out, A("BL", 128 * i, 128 * i + 128), A(src, i, n, 16), i == 0, i == 15)
+
+    def rows2list(out, src, n, kp):
+        for i in range(16):
+            mm(out, A("SelL", 128 * i, 128 * i + 128, p1=kp), A(src, i, n, 16, p1=kp), i == 0, i == 15)
+
+    def chsum(buf, w, cs=range(6), stop=False):
+        for c in cs:
+            mm(A("pb4", 16 * c, 16 * c + 16), A(buf, 128 * c, 128 * c + 128), A(w), False, stop and c == 5)
+
+    def ftsum(col, w):
+        for c in range(6):
+            mm(A("pb6", col + 16 * c, col + 16 * c + 16), A("FB", 128 * c, 128 * c + 128), A(w), True, True)
+
+    dma("s", A("R", 0, G), HB(T.reach[:, 0:G])); dma("y", A("ci"), HB(T.cand[:]))
+    dma("s", A("P", 0, G), HB(T.past[:, 0:G])); dma("y", A("X"), HB(T.x[:]))
+    dma("s", A("R", G, V), HB(T.reach[:, G:V])); dma("y", A("thr", p1=1), HB(T.th[:]))
+    dma("s", A("P", G, V), HB(T.past[:, G:V])); dma("y", A("si"), HB(T.succ[:]))
+    dma("y", A("RF", 0, V), HB(T.reach[:])); dma("y", A("PF", 0, V), HB(T.past[:]))
+
+    iota(A("pi"), [[0, 1]], 0, 1)
+    ms(A("ones"), 1.0)
+    iota(A("gmi"), [[0, 2], [1, 8]], 0, 0)
+    iota(A("mi16"), [[1, 16]], 0, 0, True)
+    iota(A("mI"), [[1, 128]], 0, 0)
+    iota(A("VL", 0, 16), [[64, 16]], 0, 0, True); iota(A("VL", 16, 32), [[16, 16]], 1024, 0, True)
+    send(A("R", 0, G), A("RF", V, V + G), A("RF", V + G, W), "iR", "li")
+    send(A("P", 0, G), A("PF", V, V + G), A("PF", V + G, W), "iP", "li")
+    arrive("iR", 2 * ne, [A("RF", V, W)]); arrive("iP", 2 * ne, [A("PF", V, W)])
+    sel(A("xF", 0, V), A("X"), [[0, 256], [1, 4]], ALU.not_equal, BIGX, 0, 0)
+    ts(A("gi"), A("pi"), 4, ALU.arith_shift_right); ts(A("ii"), A("pi"), 15, ALU.bitwise_and)
+    ts(A("ei"), A("gi"), 1, ALU.bitwise_and)
+    cp("v", A("modd"), A("ei")); cp("v", A("iF"), A("ii")); cp("v", A("gf"), A("gi")); cp("v", A("gm"), A("gmi"))
+    ts(A("meven"), A("modd"), -1.0, ALU.mult, 1.0, ALU.add)
+    ts(A("gm"), A("gm"), A("gf"), ALU.is_equal)
+    ts(A("selD"), A("gm"), 1024.0, ALU.mult); ts(A("selO"), A("gm"), 8388608.0, ALU.mult)
+    ms(A("xF", V, W), BIGX)
+    ms(A("cb", 0, 1), -10.0 * EQ); ms(A("cb", 1, 2), 1.0)
+    ts(A("mi16"), A("mi16"), A("iF"), ALU.is_equal)
+    ts(A("sj"), A("mi16"), -2.0, ALU.mult, 1.0, ALU.add)
+    ts(A("il1"), A("iF"), 10.0, ALU.is_lt)
+    ts(A("IB", 0, 1), A("il1"), -1.0, ALU.mult)
+    ms(A("EK"), 0.0)
+    ts(A("mG"), A("mI"), 4, ALU.arith_shift_right); cp("v", A("mGf"), A("mG")); ts(A("B16"), A("mGf"), A("gf"), ALU.is_equal)
+    ts(A("CfE", 0, 256), A("ci", 0, V, 4), A("meven"), ALU.mult)
+    ts(A("CfO", 0, 256), A("ci", 0, V, 4), A("modd"), ALU.mult)
+    for i in range(16):
+        cp("s" if i < 11 else "v", A("D1", i, 512, 32), A("CfE", i, 256, 16))
+    for i in range(16):
+        cp("v", A("D1", 16 + i, 512, 32), A("CfO", i, 256, 16))
+    turn()
+    dup("s", "xv2", "X", 0)
+    for k in range(16):
+        cp("s", A("EK", 128 * k + k, 128 * k + 128, 16), A("B16", k, 128, 16))
+    for j in range(10):
+        act(A("IB", 2 ** j, 2 ** (j + 1)), A("IB", 0, 2 ** j), AF.Copy, scale=A("sj", j, j + 1))
+    for k in range(16):
+        tt(A("ckf", 16 * k, 16 * k + 16), A("T1", k, 512, 32), A("T1", 16 + k, 512, 32), ALU.add)
+    cp("v", A("CK0"), A("ckf"))
+    for kk in range(8):
+        xgather(0, kk); xabs(kk)
+    halves(0, 0); halves(0, 1)
+    for n in ("SA", "SB", "SN"):
+        ms(A(n, p1=34), 0.0)
+    ms(A("rows2"), 0.0); ms(A("rows2", p0=32, p1=64), 1.0)
+    ms(A("SelL", p1=16), 0.0)
+    ms(A("rst"), 0.0)
+    sel(A("E0"), A("ones", 0, 128), [[0, 128]], ALU.is_equal, 0.0, 0, 1)
+    iota(A("kc"), [[64, 16], [0, 32]], 0, 0, True)
+    for hv in range(4):
+        sel(A("RH", 512 * hv, 512 * hv + 512), A("ones"), [[-1, 16], [-16, 16], [4096, 2]], ALU.is_equal, 0.0, 128 * (hv % 2) - 4096 * (hv // 2), 1)
+    sel(A("I"), A("ones", 0, 128), [[-1, 128]], ALU.is_equal, 0.0, 0, 1)
+    ts(A("nI"), A("I"), -1.0, ALU.mult)
+    op("g", lambda e: e.partition_broadcast(A("thb")[0], A("thr", p1=1)[0], 128), [A("thr")], [A("thb")])
+    iota(A("VR"), [[0, 6], [1, 2], [0, 8]], 0, 0, True); iota(A("CC"), [[128, 6], [0, 16]], 128, 0, True)
+    keyinit()
+    for kk in range(8):
+        keymm(kk, "ab", "selD")
+
+    def later():
+        ms(A("pw"), 0.0)
+        for i in range(10):
+            ms(A("pw", i, i + 1), 2.0 ** (i - 1))
+        tt(A("mp"), A("mi16"), A("pw"), ALU.mult); rsum(A("wcol"), A("mp"))
+        ms(A("zb"), 0.0)
+        for base in (0, 128):
+            sel(A("SelL", p1=16), A("SelL", p1=16), [[-1, 16], [1, 128]], ALU.not_equal, 1.0, base, -16)
+        iota(A("rows2", p0=32, p1=33), [[1, 256]], 0, 0, True)
+        for n, r0, i, w in (("SA", 0, 10, 1.0), ("SA", 8, 11, 1.0), ("SB", 0, 13, -4096.0), ("SB", 8, 14, -256.0)):
+            sel(A(n, p1=34), A(n, p1=34), [[1, 128]], ALU.not_equal, w, 16 * r0 - i, -16)
+        for n, d, i, w in (("SA", 0, 12, 1.0), ("SA", 1, 13, 1.0), ("SA", 1, 14, 1.0), ("SA", 1, 15, 1.0), ("SB", 1, 10, 4096.0), ("SB", 1, 11, 256.0), ("SB", 1, 12, 1.0), ("SB", 0, 15, -1.0)):
+            sel(A(n, p0=32, p1=34), A(n, p0=32, p1=34), [[0, 8], [1, 16]], ALU.not_equal, w, -i - 1000 * d, 1000)
+        sel(A("SN", p1=34), A("SN", p1=34), [[1, 8], [0, 16]], ALU.not_equal, -32768.0, 16, -1)
+        sel(A("rst"), A("rst"), [[0, 64], [1, 16]], ALU.not_equal, 1000.0, 0, 0)
+        sel(A("U"), A("ones", 0, 128), [[1, 128]], ALU.is_ge, 0.0, 0, -1)
+        dma("y", A("FB", 0, V), A("IB"))
+        ts(A("bI"), A("I"), EQ, ALU.mult)
+        ts(A("oki"), A("ii"), 1, ALU.bitwise_and); cp("v", A("okc"), A("oki")); ts(A("ekc"), A("okc"), -1.0, ALU.mult, 1.0, ALU.add)
+        for h in (0, 1):
+            ts(A("thK", h, 16, 2), A("thb"), 1024.0, ALU.mult)
+        cp("v", A("thC"), A("thK"))
+        ts(A("i4c"), A("iF"), 4.0, ALU.mult)
+        ts(A("VL", 16, 32), A("VL", 16, 32), A("iF"), ALU.add)
+        for t in (1, 2, 3):
+            ts(A("VL", 32 * t, 32 * t + 16), A("VL", 0, 16), A("i4c"), ALU.add, float(t), ALU.add)
+            cp("v", A("VL", 32 * t + 16, 32 * t + 32), A("VL", 16, 32))
+        ts(A("VL", 0, 16), A("VL", 0, 16), A("i4c"), ALU.add)
+        cp("v", A("SO"), A("si"))
+        cp("v", A("CF"), A("ci"))
+
+    def later1():
+        act(A("SE"), A("SO"), AF.Copy, scale=A("ekc"))
+        act(A("SO"), A("SO"), AF.Copy, scale=A("okc"))
+        cp("v", A("SL0"), A("si", 0, V, 2))
+        act(A("CfE"), A("CF"), AF.Copy, scale=A("meven")); act(A("CfO"), A("CF"), AF.Copy, scale=A("modd"))
+        cp("s", A("SLB", 0, 128), A("IB", G, G + 128))
+        cklist_d(1)
+
+    def later2():
+        cp("v", A("SL1"), A("si", 1, V, 2))
+        cp("v", A("pf"), A("pi"))
+        ts(A("c7"), A("iF"), 7.0, ALU.is_lt); tt(A("wlo"), A("c7"), A("wcol"), ALU.mult); tt(A("whi"), A("wcol"), A("wlo"), ALU.subtract)
+        ts(A("c8"), A("iF"), 8.0, ALU.is_ge); tt(A("fhc"), A("c8"), A("il1"), ALU.mult)
+        ts(A("wF"), A("wcol"), 16384.0, ALU.mult); ts(A("wFn"), A("wcol"), -16384.0, ALU.mult)
+        cp("v", A("selp"), A("gm")); ts(A("seln"), A("gm"), -1.0, ALU.mult)
+        for o, w in (("sFp", "wF"), ("sFn", "wFn"), ("FH", "fhc")):
+            ts(A(o), A("gm"), A(w), ALU.mult)
+        ts(A("FS", 0, 8), A("gm", 0, 8), A("wlo"), ALU.mult); ts(A("FS", 8, 16), A("gm", 8, 16), A("whi"), ALU.mult)
+        ts(A("V0"), A("VR"), -1.0, ALU.mult, 1.0, ALU.add)
+        tt(A("NG"), A("VR"), A("CC"), ALU.mult); ts(A("NG1"), A("V0"), A("pf"), ALU.mult); tt(A("NG"), A("NG"), A("NG1"), ALU.add); tt(A("NG1"), A("NG"), A("V0"), ALU.add)
+        ftsum(0, "FS"); cp("v", A("FpT"), A("pb6", 0, 96))
+        for s, d in (("RF", "GR"), ("PF", "GP")):
+            dma("y", A(d + "a", 0, G), A(s, V, V + G)); dma("y", A(d + "b", 0, G), A(s, V + G, W))
+
+    for t in range(ROUNDS):
+        last = t == ROUNDS - 1
+        ckt = "CK%d" % t; u = t + 1
+        if t == 0:
+            dup("s", "Pv2", "P", t); dup("s", "Rv2", "R", t)
+        for kk in range(8):
+            s = (512 * kk, 512 * kk + 512); off = A(ckt, 32 * kk, 32 * kk + 32)
+            tt(A("oR", *s), IND(A("RF"), off), A("Pv2"), ALU.is_le)
+            if kk not in NS_P:
+                tt(A("oP", *s), IND(A("PF"), off), A("Rv2"), ALU.is_ge)
+
+        def pgather(kk):
+            s = (512 * kk, 512 * kk + 512)
+            cp("s", A("pc", *s), IND(A("PF"), A(ckt, 32 * kk, 32 * kk + 32)))
+            bank = A("pb%d" % (2 + kk % 2))
+            mm(bank, A("I"), A("pc", *s), True, False); mm(bank, A("nI"), A("Rv2"), False, True)
+
+        def olist(kk):
+            for k in (2 * kk, 2 * kk + 1):
+                for n in ("oR", "oP"):
+                    mm(A("pb7", 0, 256), A("EK", 128 * k, 128 * k + 128), A(n, 256 * k, 256 * k + 256), k == 0 and n == "oR", False)
+        pgather(NS_P[0])
+        if t == 0:
+            later()
+        for kk in range(8):
+            if kk in NS_P:
+                if kk + 1 in NS_P:
+                    pgather(kk + 1)
+                act(A("oP", 512 * kk, 512 * kk + 512), A("pb%d" % (2 + kk % 2)), AF.Relu, bias=A("cb", 1, 2))
+            if t == 0 and kk == 7:
+                act(A("BL"), A("EK"), AF.Copy, scale=A("wcol"))
+            keymm(kk, "oR", "selO"); keymm(kk, "oP", "selO", kk in (3, 7))
+            if kk:
+                olist(kk - 1)
+        olist(7)
+        cp("s", A("ka"), A("pb0", 0, 256))
+        tt(A("t1"), A("pb1", 0, 256), A("ka"), ALU.min)
+        tt(A("wk", 0, 128), A("t1", 0, 128), A("t1", 128, 256), ALU.min)
+        tt(A("wk", 128, 192), A("wk", 0, 64), A("wk", 64, 128), ALU.min)
+        tt(A("wk", 192, 224), A("wk", 128, 160), A("wk", 160, 192), ALU.min)
+        m0 = A("wk", 192, 208)
+        cp("v", A("wi", 0, 32), A("wk", 192, 224))
+        ts(A("wk", 224, 240), m0, HASLIM, ALU.is_lt, 64.0, ALU.mult)
+        ts(A("wk", 240, 256), m0, HASLIM, ALU.is_lt)
+        ts(A("wi", 32, 64), A("wi", 0, 32), 63, ALU.bitwise_and)
+        tt(A("dec"), A("wi", 32, 64), A("wk", 224, 256), ALU.mult)
+        for h in (0, 1):
+            mm(A("pb5", 128 * h, 128 * h + 128, p1=16), A("dec", h, 32, 2), A("I"), True, True)
+        cp("s", A("rowsN", p1=16), A("pb5", 0, 256, p1=16))
+        rows2list(A("pb6", 0, 16), "rowsN", 256, 16)
+        tt(A("wk", 272, 288), m0, A("thC"), ALU.is_ge)
+        ts(A("wk", 304, 320), m0, 4095.0 * 1024, ALU.min)
+        ts(A("wk", 288, 304), A("wk", 272, 288), 4095.0 * 1024, ALU.mult)
+        ts(A("dec2", 32, 48), m0, HASLIM, ALU.is_ge)
+        tt(A("wi", 64, 80), A("wk", 288, 304), A("wk", 304, 320), ALU.max)
+        ts(A("wi", 80, 96), A("wi", 64, 80), 14, ALU.arith_shift_right)
+        ts(A("wi", 112, 128), A("wi", 64, 80), 10, ALU.arith_shift_right)
+        ts(A("wi", 96, 112), A("wi", 112, 128), 15, ALU.bitwise_and)
+        cp("v", A("dec2", 0, 32), A("wi", 80, 112))
+        for h in (0, 1):
+            mm(A("pb2", 128 * h, 128 * h + 128, p1=24), A("dec2", h, 48, 2), A("I"), True, True)
+        cp("s", A("rows2", p1=24), A("pb2", 0, 256, p1=24))
+        cp("v", A("nl"), A("pb6", 0, 16))
+        cp("v", A("bits"), IND(A("FB", 0, V), A("nl")))
+        mm(A("pb5", 0, 256), A("SA", p1=34), A("rows2", p1=34), True, False); mm(A("pb6", 0, 256), A("SB", p1=34), A("rows2", p1=34), True, False)
+        mm(A("pb5", 0, 256), A("I"), A("bits"), False, True); mm(A("pb6", 0, 256), A("bI"), A("bits"), False, True)
+        if not last:
+            halves(u, 0)
+        ts(A("Ae"), A("pb5", 0, 256), A("meven"), ALU.mult)
+        cp("s", A("Bk"), A("pb6", 0, 256))
+        ts(A("Ao"), A("pb5", 0, 256), A("modd"), ALU.mult)
+        for gp in range(4):
+            for e in (0, 1):
+                for h in (0, 1):
+                    mm(A("pb%d" % (2 * h + gp % 2), 256 * e, 256 * e + 256), A(("Ae", "Ao")[e], 128 * h, 128 * h + 128, p0=32 * gp, p1=32 * gp + 32), A("Bk", p0=32 * gp, p1=32 * gp + 32), True, True)
+            for e in (0, 1):
+                gg = 2 * gp + e
+                bk = A("pb%d" % (gp % 2), 256 * e, 256 * e + 256)
+                op("v", lambda q, bk=bk, gg=gg: q.tensor_reduce(out=A("mx", gg, gg + 1)[0], in_=bk[0], axis=AxisListType.X, op=ALU.max), [bk], [A("mx", gg, gg + 1)])
+                act(A("tr", 256 * e, 256 * e + 256), A("pb%d" % (2 + gp % 2), 256 * e, 256 * e + 256), AF.Relu, bias=A("cb", 0, 1), accum=A("mx", 8 + gg, 9 + gg))
+        bits2list(A("pb5", 0, 16), "bits", 256)
+        mm(A("pb7", 0, 256), A("SN", p1=34), A("rows2", p1=34), False, True)
+        ts(A("wk", 320, 336), A("wk", 272, 288), -1.0, ALU.mult, 1.0, ALU.add)
+        ts(A("bl"), A("pb5", 0, 16), 511.5, ALU.add)
+        ts(A("wk", 336, 352, 2), A("mx", 0, 8), 10.0 * EQ, ALU.is_le)
+        ts(A("wk", 337, 352, 2), A("mx", 8, 16), 0.0, ALU.is_le)
+        tt(A("win"), A("wk", 336, 352), A("wk", 320, 336), ALU.mult)
+        for d, bank in ((0, "pb5"), (256, "pb0")):
+            for h in (0, 1):
+                mm(A(bank, 128 * h, 128 * h + 128, p1=8), A("win", h, 16, 2), A("I"), True, True)
+        tt(A("bd", 0, 16), A("bl"), A("VL", 32 * t, 32 * t + 16), ALU.subtract); tt(A("bd", 16, 32), A("bl"), A("VL", 32 * t + 16, 32 * t + 32), ALU.subtract)
+        cp("s", A("rowsW", 0, 256, p1=8), A("pb5", 0, 256, p1=8)); cp("v", A("rowsW", 256, 512, p1=8), A("pb0", 0, 256, p1=8))
+        rows2list(A("pb6", 0, 32), "rowsW", 512, 8)
+        if t == 0:
+            later1()
+        cp("v", A("bu"), A("bl"))
+        ts(A("oi"), A("pb7", 0, 256), 0.0, ALU.is_gt)
+        tt(A("dC"), IND(A("CF"), A("bu")), A("ci", t, V, 4), ALU.subtract)
+        tt(A("bq"), A("pb6", 0, 32), A("bd"), ALU.mult)
+        tt(A("bq2"), A("bq"), A("VL", 32 * t, 32 * t + 32), ALU.add)
+        cp("v", A("LL"), A("bq2"))
+        be, bt = A("LL", 0, 16), A("LL", 16, 32)
+        if not last:
+            if t == 0:
+                later2()
+            mm(A("pb4", 0, 96), A("zb"), A("rst", 0, 96), True, False)
+            chsum("R", "selp"); chsum("P", "seln"); chsum("FB", "sFn")
+        cp("v", IND(A("FB"), bt), A("IB", t, V, 4))
+        bits2list(A("pb5", 0, 64), "FB", V)
+        tt(A("Rn"), IND(A("R"), be), A("Rv2", 0, 256), ALU.min)
+        cp("s", A("R", t, V, 4), A("Rn"))
+        tt(A("sn"), IND(A("SO"), be), A("SE", t, V, 4), ALU.add)
+        cp("v", A("SL%d" % (t % 2), t // 2, 512, 2), A("sn"))
+        ts(A("FL"), A("pb5", 0, 64), 511.5, ALU.add)
+        cp("v", A("RF", 0, 512), IND(A("R"), A("FL", 0, 32))); cp("s", A("RF", 512, V), IND(A("R"), A("FL", 32, 64)))
+        par = t % 2
+
+        def g3(q, c):
+            cp(q, A("g3", 1024 * c, 1024 * c + 1024), IND(A("RF"), A("SL%d" % par, 64 * c, 64 * c + 64)))
+
+        def s3(c):
+            s = (1024 * c, 1024 * c + 1024)
+            op("v", lambda e: e.tensor_tensor_scan(out=A("s3", *s)[0], data0=A("rst")[0], data1=A("g3", *s)[0], initial=0.0, op0=ALU.max, op1=ALU.min), [A("rst"), A("g3", *s)], [A("s3", *s)])
+        tt(A("xs"), IND(A("X"), be), A("xv2", 0, 256), ALU.add)
+        if not last:
+            tt(A("Pn"), IND(A("P"), be), A("Pv2", 0, 256), ALU.max)
+        for c in range(NV3, 8):
+            g3("s", c)
+            if c == NV3 and not last:
+                cp("s", A("P", t, V, 4), A("Pn"))
+        ts(A("xi"), A("xs"), -0.5, ALU.add, 0.5, ALU.mult)
+        cp("v", A("X", t, V, 4), A("xi"))
+        if last:
+            dma("y", HB(T.yx[:]), A("X"))
+        else:
+            sel(A("xm"), A("X"), [[0, 256], [1, 4]], ALU.not_equal, BIGX, -u, 0)
+        tt(A("oi"), A("oi"), A("dC"), ALU.mult)
+        tt(A("CF", t, V, 4), A("oi"), A("CF", t, V, 4), ALU.add)
+        if last:
+            dma("y", HB(T.yc[:]), A("CF"))
+        for c in range(NV3):
+            g3("v", c)
+        if not last:
+            mm(A("pb6", 192, 208), A("ones", 0, 128), A("win"), True, True)
+            ftsum(0, "FS"); ftsum(96, "FH")
+            chsum("FB", "sFp"); chsum("P", "selp")
+            rsum(A("Mf"), A("pb6", 192, 208))
+            ts(A("xw", 0, 96), A("pb6", 96, 192), 1.0, ALU.is_lt)
+            tt(A("dF"), A("pb6", 0, 96), A("FpT"), ALU.subtract)
+            tt(A("dF"), A("dF"), A("xw", 0, 96), ALU.mult)
+            cklist_t()
+        for j in range(4):
+            s3(2 * j); s3(2 * j + 1)
+            o = A("R", par + 256 * j, 256 * j + 256, 2)
+            tt(o, A("s3", 2048 * j + 15, 2048 * j + 2048, 16), o, ALU.min)
+            if not last and j < 3:
+                chsum("R", "seln", (2 * j, 2 * j + 1), j == 2)
+            if last and j % 2:
+                dma("sy"[j // 2], HB(T.yr[:, 256 * j - 256:256 * j + 256]), A("R", 256 * j - 256, 256 * j + 256))
+        if last:
+            break
+        cp("s", A("xF", 0, V), IND(A("xm"), A("FL")))
+        dup("s", "xv2", "X", u)
+        ts(A("ch"), A("pb4", 0, 96), 0.0, ALU.not_equal)
+        mm(A("pb5", 0, 96), A("U"), A("ch"), True, False)
+        for s in range(1, 6):
+            mm(A("pb5", 16 * s, 96), A("ones", 0, 128), A("ch", 0, 96 - 16 * s), False, s == 5)
+        ts(A("xw", 0, 96), A("pb5", 0, 96), 128.0, ALU.is_le)
+        tt(A("xw", 192, 288), A("pb5", 0, 96), A("V0"), ALU.mult)
+        tt(A("xw", 96, 192), A("xw", 0, 96), A("ch"), ALU.mult)
+        tt(A("xw", 288, 384), A("xw", 192, 288), A("NG1"), ALU.subtract)
+        tt(A("xw", 384, 480), A("xw", 288, 384), A("xw", 96, 192), ALU.mult)
+        tt(A("pos"), A("xw", 384, 480), A("NG"), ALU.add)
+
+        def torows(src, rows, b0, b1, q):
+            for c in range(6):
+                bank, o = ((b0, 128 * c) if c < 4 else (b1, 128 * c - 512))
+                mm(A(bank, o, o + 128, p1=16), A(src, 16 * c, 16 * c + 16), A("I"), True, True)
+            cp("s", A(rows, 0, 512, p1=16), A(b0, 0, 512, p1=16)); cp(q, A(rows, 512, G, p1=16), A(b1, 0, 256, p1=16))
+        tt(A("xw", 480, 576), A("dF"), A("xw", 96, 192), ALU.mult)
+        torows("pos", "rowsP", "pb5", "pb6", "v")
+        rows2list(A("pb7", 0, 48), "rowsP", G, 16)
+        cp("v", A("CK%d" % u), A("ckf"))
+        tt(A("FpT"), A("FpT"), A("xw", 480, 576), ALU.add)
+        cp("v", A("Fpb"), A("FpT"))
+        xgather(u, 0)
+        cp("v", A("pl"), A("pb7", 0, 48))
+        torows("Fpb", "rowsF", "pb2", "pb3", "s")
+        rows2list(A("pb5", 0, 48), "rowsF", G, 16)
+        cp("v", IND(A("SLB"), A("pl")), A("IB", 0, G))
+        bits2list(A("pb7", 0, 8), "SLB", 128)
+        sp, sll = "SRP%d" % t, "SLL%d" % t
+        ts(A(sll, 8, 56), A("pb5", 0, 48), 511.5, ALU.add)
+        xabs(0)
+        ts(A(sll, 0, 8), A("pb7", 0, 8), 511.5, ALU.add)
+        cp("v", A(sp, 0, 128), IND(A("R"), A(sll, 0, 8))); cp("s", A(sp, 128, 256), IND(A("P"), A(sll, 0, 8)))
+        send(A(sll), A("LLa%d" % t), A("LLb%d" % t), "aL%d" % t)
+        send(A(sp), A("LRa%d" % t), A("LRb%d" % t), "aR%d" % t)
+        arrive("aR%d" % t, 2 * ne, [A("LRa%d" % t), A("LRb%d" % t)]); arrive("aL%d" % t, 2 * ne, [A("LLa%d" % t), A("LLb%d" % t)])
+        cp("s", A("SLB", 0, 128), A("IB", G, G + 128))
+        cp("s", A("RF", 0, V), IND(A("R"), A("FL")))
+        for kk in range(1, 8):
+            if kk in NX_S:
+                s, bank = (512 * kk, 512 * kk + 512), A("pb%d" % (2 + kk % 2))
+                cp("s", A("dx", *s), IND(A("xF"), A("CK%d" % u, 32 * kk, 32 * kk + 32)))
+                mm(bank, A("I"), A("dx", *s), True, False); mm(bank, A("nI"), A("xv2"), False, True)
+            else:
+                xgather(u, kk)
+        for kk in range(1, 8):
+            if kk in NX_S:
+                act(A("ab", 512 * kk, 512 * kk + 512), A("pb%d" % (2 + kk % 2)), AF.Abs)
+            else:
+                xabs(kk)
+        cp("s", A("PF", 0, V), IND(A("P"), A("FL")))
+        dup("s", "Pv2", "P", u); dup("s", "Rv2", "R", u)
+        act(A("SO", t, V, 4), A("sn"), AF.Copy, scale=A("okc"))
+        halves(u, 1)
+        keyinit()
+        for kk in range(8):
+            keymm(kk, "ab", "selD")
+        cp("v", A("Mi"), A("Mf")); ts(A("Mj"), A("Mi"), 31, ALU.bitwise_and); ts(A("Mk"), A("Mj"), 1024.0, ALU.mult)
+        ts(A("thC"), A("thK"), A("Mk"), ALU.add)
+        if u + 1 < ROUNDS:
+            cklist_d(u + 1)
+        ll = {d: "LL%s%d" % (d, t) for d in "ab"}
+        for k, tb in ((1, "GP"), (0, "GR")):
+            for d in "ab":
+                cp("v", IND(A(tb + d), A(ll[d], 0, 8)), A("LR%s%d" % (d, t), 128 * k, 128 * k + 128))
+        for k, d in enumerate("ab"):
+            cp("s", A("PF", V + G * k, V + G * k + G), IND(A("GP" + d), A(ll[d], 8, 56)))
+        cp("v", A("RF", V, V + G), IND(A("GRa"), A(ll["a"], 8, 56)))
+        cp("v", A("RF", V + G, V + G + 384), IND(A("GRb"), A(ll["b"], 8, 32)))
+        cp("s", A("RF", V + G + 384, W), IND(A("GRb"), A(ll["b"], 32, 56)))
+
+    for s, v in total.items():
+        g.wait_ge(T.sem[s], v)

@@ -6,8 +6,8 @@ V, G, W, N, ROUNDS = 1024, 768, 2560, 4, 4
 BIGX = 8192.0
 HASLIM = 4100.0 * 1024
 EQ = 1048576.0
-NS_P = (2, 3, 4, 5, 6, 7)
-NX_S = (6, 7)
+NS_P = ((0, 1, 2, 3, 4, 5, 6, 7),) + ((3, 4, 5, 6, 7),) * 3
+NX_S = ()
 NV3 = 1
 
 b, f, i4, u2 = "bfloat16", "float32", "int32", "uint16"
@@ -24,8 +24,8 @@ _S = {
     "gmi": (16, i4), "mi16": (16, f), "mp": (16, f), "pw": (16, f), "sj": (16, f),
     "pi": (1, i4), "gi": (1, i4), "ii": (1, i4), "ei": (1, i4), "oki": (1, i4), "mI": (128, i4), "mG": (128, i4), "mGf": (128, f),
     "pf": (1, f), "gf": (1, f), "iF": (1, f), "i4c": (1, f), "modd": (1, f), "meven": (1, f), "okc": (1, f), "ekc": (1, f),
-    "wcol": (1, f), "il1": (1, f), "wlo": (1, f), "whi": (1, f), "wF": (1, f), "wFn": (1, f), "fhc": (1, f), "c7": (1, f), "c8": (1, f),
-    "cb": (2, f), "VL": (128, f), "VR": (96, f), "CC": (96, f), "V0": (96, f), "NG": (96, f), "NG1": (96, f),
+    "wcol": (1, f), "il1": (1, f), "wlo": (1, f), "whi": (1, f), "wF": (1, f), "wFn": (1, f), "fhc": (1, f), "c7": (1, f), "c8": (1, f), "mone": (1, f), "c64": (1, f),
+    "cb": (2, f), "VL": (128, f), "VR": (96, f), "CC": (96, f), "V0": (96, f), "NG": (96, b), "NG1": (96, b), "kI": (128, b), "chz": (96, b), "thT": (16, f), "thA": (16, f),
     "thr": (8, i4), "thb": (8, i4), "thK": (16, f), "thC": (16, f), "Mf": (1, f), "Mi": (1, i4), "Mj": (1, i4), "Mk": (1, f),
     "xv2": (512, b), "Rv2": (512, b), "Pv2": (512, b), "dx": (4096, b), "ab": (4096, b), "oR": (4096, b), "oP": (4096, b), "pc": (4096, b),
     "ka": (256, f), "t1": (256, f), "wk": (512, f), "wi": (128, i4), "dec": (32, b), "dec2": (48, b), "rowsN": (256, b), "nl": (16, u2),
@@ -217,6 +217,11 @@ def rank_program(g, core, T, topo):
         s = (512 * kk, 512 * kk + 512)
         tt(A("dx", *s), IND(A("xF"), A("CK%d" % t, 32 * kk, 32 * kk + 32)), A("xv2"), ALU.subtract)
 
+    def xscalar(t, kk):
+        s, bank = (512 * kk, 512 * kk + 512), A("pb%d" % (2 + kk % 2))
+        cp("s", A("dx", *s), IND(A("xF"), A("CK%d" % t, 32 * kk, 32 * kk + 32)))
+        mm(bank, A("I"), A("dx", *s), True, False); mm(bank, A("nI"), A("xv2"), False, True)
+
     def xabs(kk):
         s = (512 * kk, 512 * kk + 512)
         act(A("ab", *s), A("dx", *s), AF.Abs)
@@ -278,6 +283,7 @@ def rank_program(g, core, T, topo):
     ms(A("cb", 0, 1), -10.0 * EQ); ms(A("cb", 1, 2), 1.0)
     ts(A("mi16"), A("mi16"), A("iF"), ALU.is_equal)
     ts(A("sj"), A("mi16"), -2.0, ALU.mult, 1.0, ALU.add)
+    ts(A("c64"), A("iF"), 8.0, ALU.is_lt, 63.0, ALU.mult); ts(A("c64"), A("c64"), 1.0, ALU.add)
     ts(A("il1"), A("iF"), 10.0, ALU.is_lt)
     ts(A("IB", 0, 1), A("il1"), -1.0, ALU.mult)
     ms(A("EK"), 0.0)
@@ -297,20 +303,24 @@ def rank_program(g, core, T, topo):
     for k in range(16):
         tt(A("ckf", 16 * k, 16 * k + 16), A("T1", k, 512, 32), A("T1", 16 + k, 512, 32), ALU.add)
     cp("v", A("CK0"), A("ckf"))
-    for kk in range(8):
-        xgather(0, kk); xabs(kk)
+    for kk in range(7):
+        xgather(0, kk)
     halves(0, 0); halves(0, 1)
-    for n in ("SA", "SB", "SN"):
-        ms(A(n, p1=34), 0.0)
-    ms(A("rows2"), 0.0); ms(A("rows2", p0=32, p1=64), 1.0)
-    ms(A("SelL", p1=16), 0.0)
-    ms(A("rst"), 0.0)
+    dma("y", A("SelL", p1=8), (T.EK[0:128:16, :], A("EK")[1])); dma("y", A("SelL", p0=8, p1=16), (T.EK[0:128:16, :], A("EK")[1]))
+    ms(A("rows2"), 0.0)
     sel(A("E0"), A("ones", 0, 128), [[0, 128]], ALU.is_equal, 0.0, 0, 1)
     iota(A("kc"), [[64, 16], [0, 32]], 0, 0, True)
     for hv in range(4):
         sel(A("RH", 512 * hv, 512 * hv + 512), A("ones"), [[-1, 16], [-16, 16], [4096, 2]], ALU.is_equal, 0.0, 128 * (hv % 2) - 4096 * (hv // 2), 1)
     sel(A("I"), A("ones", 0, 128), [[-1, 128]], ALU.is_equal, 0.0, 0, 1)
-    ts(A("nI"), A("I"), -1.0, ALU.mult)
+    sel(A("nI"), A("I"), [[-1, 128]], ALU.not_equal, -1.0, 0, 1)
+    xscalar(0, 7)
+    for kk in range(7):
+        xabs(kk)
+    act(A("ab", 3584, 4096), A("pb3"), AF.Abs)
+    iota(A("SN", p1=65), [[0, 128]], 0, 0, True)
+    sel(A("SN", p1=65), A("SN", p1=65), [[1, 8], [0, 16]], ALU.not_equal, -32768.0, 16, -1)
+    iota(A("rows2", p0=32, p1=33), [[1, 256]], 0, 0, True)
     op("g", lambda e: e.partition_broadcast(A("thb")[0], A("thr", p1=1)[0], 128), [A("thr")], [A("thb")])
     iota(A("VR"), [[0, 6], [1, 2], [0, 8]], 0, 0, True); iota(A("CC"), [[128, 6], [0, 16]], 128, 0, True)
     keyinit()
@@ -318,20 +328,22 @@ def rank_program(g, core, T, topo):
         keymm(kk, "ab", "selD")
 
     def later():
+        cp("v", A("CF"), A("ci"))
         ms(A("pw"), 0.0)
         for i in range(10):
             ms(A("pw", i, i + 1), 2.0 ** (i - 1))
         tt(A("mp"), A("mi16"), A("pw"), ALU.mult); rsum(A("wcol"), A("mp"))
         ms(A("zb"), 0.0)
-        for base in (0, 128):
-            sel(A("SelL", p1=16), A("SelL", p1=16), [[-1, 16], [1, 128]], ALU.not_equal, 1.0, base, -16)
-        iota(A("rows2", p0=32, p1=33), [[1, 256]], 0, 0, True)
-        for n, r0, i, w in (("SA", 0, 10, 1.0), ("SA", 8, 11, 1.0), ("SB", 0, 13, -4096.0), ("SB", 8, 14, -256.0)):
-            sel(A(n, p1=34), A(n, p1=34), [[1, 128]], ALU.not_equal, w, 16 * r0 - i, -16)
-        for n, d, i, w in (("SA", 0, 12, 1.0), ("SA", 1, 13, 1.0), ("SA", 1, 14, 1.0), ("SA", 1, 15, 1.0), ("SB", 1, 10, 4096.0), ("SB", 1, 11, 256.0), ("SB", 1, 12, 1.0), ("SB", 0, 15, -1.0)):
-            sel(A(n, p0=32, p1=34), A(n, p0=32, p1=34), [[0, 8], [1, 16]], ALU.not_equal, w, -i - 1000 * d, 1000)
-        sel(A("SN", p1=34), A("SN", p1=34), [[1, 8], [0, 16]], ALU.not_equal, -32768.0, 16, -1)
-        sel(A("rst"), A("rst"), [[0, 64], [1, 16]], ALU.not_equal, 1000.0, 0, 0)
+        ms(A("rows2", p0=64, p1=65), 1.0)
+        for n in ("SA", "SB"):
+            ms(A(n, p1=65), 0.0)
+        ms(A("rst"), 0.0)
+        for n, r, i, w in (("SA", 32, 12, 1.0), ("SA", 64, 13, 1.0), ("SA", 64, 14, 1.0), ("SA", 64, 15, 1.0), ("SB", 64, 10, 4096.0), ("SB", 64, 11, 256.0), ("SB", 64, 12, 1.0), ("SB", 32, 15, -1.0)):
+            ms(A(n, i, 128, 16, p0=r, p1=r + 1), w)
+        for n, c, i, w in (("SA", 0, 10, 1.0), ("SA", 8, 11, 1.0), ("SB", 0, 13, -4096.0), ("SB", 8, 14, -256.0)):
+            ts(A(n, i, 128, 16, p1=16), A("I", c, c + 8, p1=16), w, ALU.mult)
+        ms(A("rst", 0, 1024, 16), 1000.0)
+        ms(A("thT"), 1.0); ms(A("thT", 0, 16, 2), 10.0 * EQ + 1.0)
         sel(A("U"), A("ones", 0, 128), [[1, 128]], ALU.is_ge, 0.0, 0, -1)
         dma("y", A("FB", 0, V), A("IB"))
         ts(A("bI"), A("I"), EQ, ALU.mult)
@@ -346,15 +358,12 @@ def rank_program(g, core, T, topo):
             cp("v", A("VL", 32 * t + 16, 32 * t + 32), A("VL", 16, 32))
         ts(A("VL", 0, 16), A("VL", 0, 16), A("i4c"), ALU.add)
         cp("v", A("SO"), A("si"))
-        cp("v", A("CF"), A("ci"))
 
     def later1():
         act(A("SE"), A("SO"), AF.Copy, scale=A("ekc"))
         act(A("SO"), A("SO"), AF.Copy, scale=A("okc"))
         cp("v", A("SL0"), A("si", 0, V, 2))
-        act(A("CfE"), A("CF"), AF.Copy, scale=A("meven")); act(A("CfO"), A("CF"), AF.Copy, scale=A("modd"))
         cp("s", A("SLB", 0, 128), A("IB", G, G + 128))
-        cklist_d(1)
 
     def later2():
         cp("v", A("SL1"), A("si", 1, V, 2))
@@ -362,12 +371,14 @@ def rank_program(g, core, T, topo):
         ts(A("c7"), A("iF"), 7.0, ALU.is_lt); tt(A("wlo"), A("c7"), A("wcol"), ALU.mult); tt(A("whi"), A("wcol"), A("wlo"), ALU.subtract)
         ts(A("c8"), A("iF"), 8.0, ALU.is_ge); tt(A("fhc"), A("c8"), A("il1"), ALU.mult)
         ts(A("wF"), A("wcol"), 16384.0, ALU.mult); ts(A("wFn"), A("wcol"), -16384.0, ALU.mult)
-        cp("v", A("selp"), A("gm")); ts(A("seln"), A("gm"), -1.0, ALU.mult)
-        for o, w in (("sFp", "wF"), ("sFn", "wFn"), ("FH", "fhc")):
-            ts(A(o), A("gm"), A(w), ALU.mult)
-        ts(A("FS", 0, 8), A("gm", 0, 8), A("wlo"), ALU.mult); ts(A("FS", 8, 16), A("gm", 8, 16), A("whi"), ALU.mult)
+        ms(A("mone"), -1.0)
+        cp("s", A("selp"), A("gm"))
+        for o, w in (("seln", "mone"), ("sFp", "wF"), ("sFn", "wFn"), ("FH", "fhc")):
+            act(A(o), A("gm"), AF.Copy, scale=A(w))
+        act(A("FS", 0, 8), A("gm", 0, 8), AF.Copy, scale=A("wlo")); act(A("FS", 8, 16), A("gm", 8, 16), AF.Copy, scale=A("whi"))
         ts(A("V0"), A("VR"), -1.0, ALU.mult, 1.0, ALU.add)
-        tt(A("NG"), A("VR"), A("CC"), ALU.mult); ts(A("NG1"), A("V0"), A("pf"), ALU.mult); tt(A("NG"), A("NG"), A("NG1"), ALU.add); tt(A("NG1"), A("NG"), A("V0"), ALU.add)
+        tt(A("CC"), A("VR"), A("CC"), ALU.mult); ts(A("VR"), A("V0"), A("pf"), ALU.mult); tt(A("NG"), A("CC"), A("VR"), ALU.add); tt(A("NG1"), A("NG"), A("V0"), ALU.add)
+        ts(A("kI"), A("I"), -1024.0, ALU.mult)
         ftsum(0, "FS"); cp("v", A("FpT"), A("pb6", 0, 96))
         for s, d in (("RF", "GR"), ("PF", "GP")):
             dma("y", A(d + "a", 0, G), A(s, V, V + G)); dma("y", A(d + "b", 0, G), A(s, V + G, W))
@@ -377,10 +388,13 @@ def rank_program(g, core, T, topo):
         ckt = "CK%d" % t; u = t + 1
         if t == 0:
             dup("s", "Pv2", "P", t); dup("s", "Rv2", "R", t)
-        for kk in range(8):
+        nsp = NS_P[t]; first = [True]
+
+        def vchunk(n, kk):
             s = (512 * kk, 512 * kk + 512); off = A(ckt, 32 * kk, 32 * kk + 32)
-            tt(A("oR", *s), IND(A("RF"), off), A("Pv2"), ALU.is_le)
-            if kk not in NS_P:
+            if n == "oR":
+                tt(A("oR", *s), IND(A("RF"), off), A("Pv2"), ALU.is_le)
+            else:
                 tt(A("oP", *s), IND(A("PF"), off), A("Rv2"), ALU.is_ge)
 
         def pgather(kk):
@@ -389,38 +403,49 @@ def rank_program(g, core, T, topo):
             bank = A("pb%d" % (2 + kk % 2))
             mm(bank, A("I"), A("pc", *s), True, False); mm(bank, A("nI"), A("Rv2"), False, True)
 
+        def prelu(kk):
+            act(A("oP", 512 * kk, 512 * kk + 512), A("pb%d" % (2 + kk % 2)), AF.Relu, bias=A("cb", 1, 2))
+
         def olist(kk):
             for k in (2 * kk, 2 * kk + 1):
                 for n in ("oR", "oP"):
-                    mm(A("pb7", 0, 256), A("EK", 128 * k, 128 * k + 128), A(n, 256 * k, 256 * k + 256), k == 0 and n == "oR", False)
-        pgather(NS_P[0])
+                    mm(A("pb7", 0, 256), A("EK", 128 * k, 128 * k + 128), A(n, 256 * k, 256 * k + 256), first[0], False)
+                    first[0] = False
+        work = [(n, kk) for kk in range(8) for n in ("oR", "oP") if n == "oR" or kk not in nsp]
+        ev = [(i + 1.0, 0, n, kk) for i, (n, kk) in enumerate(work)]
+        ev += [(1.7 * j + 1.0, 1, "g", kk) for j, kk in enumerate(nsp)] + [(1.7 * j + 2.8, 2, "r", kk) for j, kk in enumerate(nsp)]
+        left = {0: 16, 1: 16}
+        for _, _, n, kk in sorted(ev):
+            if n == "g":
+                pgather(kk)
+                continue
+            if n == "r":
+                prelu(kk)
+            else:
+                vchunk(n, kk)
+            n = "oP" if n == "r" else n
+            left[kk // 4] -= 2
+            keymm(kk, n, "selO", left[kk // 4] == 0)
         if t == 0:
             later()
-        for kk in range(8):
-            if kk in NS_P:
-                if kk + 1 in NS_P:
-                    pgather(kk + 1)
-                act(A("oP", 512 * kk, 512 * kk + 512), A("pb%d" % (2 + kk % 2)), AF.Relu, bias=A("cb", 1, 2))
-            if t == 0 and kk == 7:
-                act(A("BL"), A("EK"), AF.Copy, scale=A("wcol"))
-            keymm(kk, "oR", "selO"); keymm(kk, "oP", "selO", kk in (3, 7))
-            if kk:
-                olist(kk - 1)
-        olist(7)
+            act(A("CfE"), A("CF"), AF.Copy, scale=A("meven")); act(A("CfO"), A("CF"), AF.Copy, scale=A("modd"))
+            act(A("BL"), A("EK"), AF.Copy, scale=A("wcol"))
+            cklist_d(1)
+        if not last:
+            halves(u, 0); halves(u, 1)
         cp("s", A("ka"), A("pb0", 0, 256))
         tt(A("t1"), A("pb1", 0, 256), A("ka"), ALU.min)
         tt(A("wk", 0, 128), A("t1", 0, 128), A("t1", 128, 256), ALU.min)
         tt(A("wk", 128, 192), A("wk", 0, 64), A("wk", 64, 128), ALU.min)
         tt(A("wk", 192, 224), A("wk", 128, 160), A("wk", 160, 192), ALU.min)
         m0 = A("wk", 192, 208)
-        cp("v", A("wi", 0, 32), A("wk", 192, 224))
-        ts(A("wk", 224, 240), m0, HASLIM, ALU.is_lt, 64.0, ALU.mult)
-        ts(A("wk", 240, 256), m0, HASLIM, ALU.is_lt)
+        ts(A("wi", 0, 32), A("wk", 192, 224), 16777215.0, ALU.min)
+        ts(A("wk", 224, 256), A("wk", 192, 224), HASLIM, ALU.is_lt)
         ts(A("wi", 32, 64), A("wi", 0, 32), 63, ALU.bitwise_and)
         tt(A("dec"), A("wi", 32, 64), A("wk", 224, 256), ALU.mult)
         for h in (0, 1):
             mm(A("pb5", 128 * h, 128 * h + 128, p1=16), A("dec", h, 32, 2), A("I"), True, True)
-        cp("s", A("rowsN", p1=16), A("pb5", 0, 256, p1=16))
+        act(A("rowsN", p1=16), A("pb5", 0, 256, p1=16), AF.Copy, scale=A("c64", p1=16))
         rows2list(A("pb6", 0, 16), "rowsN", 256, 16)
         tt(A("wk", 272, 288), m0, A("thC"), ALU.is_ge)
         ts(A("wk", 304, 320), m0, 4095.0 * 1024, ALU.min)
@@ -436,10 +461,10 @@ def rank_program(g, core, T, topo):
         cp("s", A("rows2", p1=24), A("pb2", 0, 256, p1=24))
         cp("v", A("nl"), A("pb6", 0, 16))
         cp("v", A("bits"), IND(A("FB", 0, V), A("nl")))
-        mm(A("pb5", 0, 256), A("SA", p1=34), A("rows2", p1=34), True, False); mm(A("pb6", 0, 256), A("SB", p1=34), A("rows2", p1=34), True, False)
+        tt(A("wk", 320, 336), A("wk", 272, 288), A("thT"), ALU.mult)
+        tt(A("thA"), A("thT"), A("wk", 320, 336), ALU.subtract); ts(A("thA"), A("thA"), 1.0, ALU.subtract)
+        mm(A("pb5", 0, 256), A("SA", p1=65), A("rows2", p1=65), True, False); mm(A("pb6", 0, 256), A("SB", p1=65), A("rows2", p1=65), True, False)
         mm(A("pb5", 0, 256), A("I"), A("bits"), False, True); mm(A("pb6", 0, 256), A("bI"), A("bits"), False, True)
-        if not last:
-            halves(u, 0)
         ts(A("Ae"), A("pb5", 0, 256), A("meven"), ALU.mult)
         cp("s", A("Bk"), A("pb6", 0, 256))
         ts(A("Ao"), A("pb5", 0, 256), A("modd"), ALU.mult)
@@ -450,15 +475,11 @@ def rank_program(g, core, T, topo):
             for e in (0, 1):
                 gg = 2 * gp + e
                 bk = A("pb%d" % (gp % 2), 256 * e, 256 * e + 256)
-                op("v", lambda q, bk=bk, gg=gg: q.tensor_reduce(out=A("mx", gg, gg + 1)[0], in_=bk[0], axis=AxisListType.X, op=ALU.max), [bk], [A("mx", gg, gg + 1)])
-                act(A("tr", 256 * e, 256 * e + 256), A("pb%d" % (2 + gp % 2), 256 * e, 256 * e + 256), AF.Relu, bias=A("cb", 0, 1), accum=A("mx", 8 + gg, 9 + gg))
+                op("v", lambda q, bk=bk, gg=gg: q.tensor_reduce(out=A("mx", 2 * gg, 2 * gg + 1)[0], in_=bk[0], axis=AxisListType.X, op=ALU.max), [bk], [A("mx", 2 * gg, 2 * gg + 1)])
+                act(A("tr", 256 * e, 256 * e + 256), A("pb%d" % (2 + gp % 2), 256 * e, 256 * e + 256), AF.Relu, bias=A("cb", 0, 1), accum=A("mx", 2 * gg + 1, 2 * gg + 2))
         bits2list(A("pb5", 0, 16), "bits", 256)
-        mm(A("pb7", 0, 256), A("SN", p1=34), A("rows2", p1=34), False, True)
-        ts(A("wk", 320, 336), A("wk", 272, 288), -1.0, ALU.mult, 1.0, ALU.add)
+        tt(A("win"), A("mx"), A("thA"), ALU.is_le)
         ts(A("bl"), A("pb5", 0, 16), 511.5, ALU.add)
-        ts(A("wk", 336, 352, 2), A("mx", 0, 8), 10.0 * EQ, ALU.is_le)
-        ts(A("wk", 337, 352, 2), A("mx", 8, 16), 0.0, ALU.is_le)
-        tt(A("win"), A("wk", 336, 352), A("wk", 320, 336), ALU.mult)
         for d, bank in ((0, "pb5"), (256, "pb0")):
             for h in (0, 1):
                 mm(A(bank, 128 * h, 128 * h + 128, p1=8), A("win", h, 16, 2), A("I"), True, True)
@@ -468,7 +489,6 @@ def rank_program(g, core, T, topo):
         if t == 0:
             later1()
         cp("v", A("bu"), A("bl"))
-        ts(A("oi"), A("pb7", 0, 256), 0.0, ALU.is_gt)
         tt(A("dC"), IND(A("CF"), A("bu")), A("ci", t, V, 4), ALU.subtract)
         tt(A("bq"), A("pb6", 0, 32), A("bd"), ALU.mult)
         tt(A("bq2"), A("bq"), A("VL", 32 * t, 32 * t + 32), ALU.add)
@@ -508,10 +528,6 @@ def rank_program(g, core, T, topo):
             dma("y", HB(T.yx[:]), A("X"))
         else:
             sel(A("xm"), A("X"), [[0, 256], [1, 4]], ALU.not_equal, BIGX, -u, 0)
-        tt(A("oi"), A("oi"), A("dC"), ALU.mult)
-        tt(A("CF", t, V, 4), A("oi"), A("CF", t, V, 4), ALU.add)
-        if last:
-            dma("y", HB(T.yc[:]), A("CF"))
         for c in range(NV3):
             g3("v", c)
         if not last:
@@ -523,36 +539,53 @@ def rank_program(g, core, T, topo):
             tt(A("dF"), A("pb6", 0, 96), A("FpT"), ALU.subtract)
             tt(A("dF"), A("dF"), A("xw", 0, 96), ALU.mult)
             cklist_t()
-        for j in range(4):
-            s3(2 * j); s3(2 * j + 1)
-            o = A("R", par + 256 * j, 256 * j + 256, 2)
-            tt(o, A("s3", 2048 * j + 15, 2048 * j + 2048, 16), o, ALU.min)
-            if not last and j < 3:
-                chsum("R", "seln", (2 * j, 2 * j + 1), j == 2)
-            if last and j % 2:
-                dma("sy"[j // 2], HB(T.yr[:, 256 * j - 256:256 * j + 256]), A("R", 256 * j - 256, 256 * j + 256))
+        for kk in range(8):
+            olist(kk)
+        mm(A("pb7", 0, 256), A("SN", p1=65), A("rows2", p1=65), False, True)
+
+        def cupdate():
+            tt(A("oi"), A("oi"), A("dC"), ALU.mult)
+            tt(A("CF", t, V, 4), A("oi"), A("CF", t, V, 4), ALU.add)
+        for c0, c1 in ((0, 5), (5, 8)):
+            for c in range(c0, c1):
+                s3(c)
+            if c0 == 0 and last:
+                ts(A("oi"), A("pb7", 0, 256), 0.0, ALU.is_gt); cupdate()
+                dma("y", HB(T.yc[:]), A("CF"))
+            o = A("R", par + 128 * c0, 128 * c1, 2)
+            tt(o, A("s3", 1024 * c0 + 15, 1024 * c1, 16), o, ALU.min)
+            if not last:
+                chsum("R", "seln", range(c0, min(c1, 6)), c1 == 8)
+            else:
+                dma("sy"[c0 // 5], HB(T.yr[:, 128 * c0:128 * c1]), A("R", 128 * c0, 128 * c1))
         if last:
             break
         cp("s", A("xF", 0, V), IND(A("xm"), A("FL")))
-        dup("s", "xv2", "X", u)
+        dup("s", "xv2", "X", u); dup("s", "Pv2", "P", u)
         ts(A("ch"), A("pb4", 0, 96), 0.0, ALU.not_equal)
         mm(A("pb5", 0, 96), A("U"), A("ch"), True, False)
         for s in range(1, 6):
-            mm(A("pb5", 16 * s, 96), A("ones", 0, 128), A("ch", 0, 96 - 16 * s), False, s == 5)
-        ts(A("xw", 0, 96), A("pb5", 0, 96), 128.0, ALU.is_le)
-        tt(A("xw", 192, 288), A("pb5", 0, 96), A("V0"), ALU.mult)
-        tt(A("xw", 96, 192), A("xw", 0, 96), A("ch"), ALU.mult)
-        tt(A("xw", 288, 384), A("xw", 192, 288), A("NG1"), ALU.subtract)
-        tt(A("xw", 384, 480), A("xw", 288, 384), A("xw", 96, 192), ALU.mult)
-        tt(A("pos"), A("xw", 384, 480), A("NG"), ALU.add)
+            mm(A("pb5", 16 * s, 96), A("ones", 0, 128), A("ch", 0, 96 - 16 * s), False, False)
+        mm(A("pb5", 0, 96), A("kI"), A("ch"), False, True)
+        tt(A("chz"), A("ch"), A("V0"), ALU.mult)
+        mm(A("pb6", 0, 96), A("nI"), A("NG1"), True, False)
+        mm(A("pb6", 0, 96), A("U"), A("chz"), False, False)
+        for s in range(1, 6):
+            mm(A("pb6", 16 * s, 96), A("ones", 0, 128), A("chz", 0, 96 - 16 * s), False, s == 5)
+        cp("v", A("Mi"), A("Mf")); ts(A("Mj"), A("Mi"), 31, ALU.bitwise_and)
+        ts(A("xw", 96, 192), A("pb5", 0, 96), 128.0 - 1024.0, ALU.is_le)
+        tt(A("pos"), A("pb6", 0, 96), A("xw", 96, 192), ALU.mult)
 
-        def torows(src, rows, b0, b1, q):
+        def torows(src, rows, b0, b1, q, more=None):
             for c in range(6):
                 bank, o = ((b0, 128 * c) if c < 4 else (b1, 128 * c - 512))
-                mm(A(bank, o, o + 128, p1=16), A(src, 16 * c, 16 * c + 16), A("I"), True, True)
+                mm(A(bank, o, o + 128, p1=16), A(src, 16 * c, 16 * c + 16), A("I"), True, more is None)
+                if more is not None:
+                    mm(A(bank, o, o + 128, p1=16), A(more, 16 * c, 16 * c + 16), A("I"), False, True)
             cp("s", A(rows, 0, 512, p1=16), A(b0, 0, 512, p1=16)); cp(q, A(rows, 512, G, p1=16), A(b1, 0, 256, p1=16))
         tt(A("xw", 480, 576), A("dF"), A("xw", 96, 192), ALU.mult)
-        torows("pos", "rowsP", "pb5", "pb6", "v")
+        torows("pos", "rowsP", "pb5", "pb6", "v", "NG")
+        ts(A("oi"), A("pb7", 0, 256), 0.0, ALU.is_gt)
         rows2list(A("pb7", 0, 48), "rowsP", G, 16)
         cp("v", A("CK%d" % u), A("ckf"))
         tt(A("FpT"), A("FpT"), A("xw", 480, 576), ALU.add)
@@ -566,6 +599,8 @@ def rank_program(g, core, T, topo):
         sp, sll = "SRP%d" % t, "SLL%d" % t
         ts(A(sll, 8, 56), A("pb5", 0, 48), 511.5, ALU.add)
         xabs(0)
+        cp("s", A("PF", 0, V), IND(A("P"), A("FL")))
+        ts(A("Mk"), A("Mj"), 1024.0, ALU.mult); ts(A("thC"), A("thK"), A("Mk"), ALU.add)
         ts(A(sll, 0, 8), A("pb7", 0, 8), 511.5, ALU.add)
         cp("v", A(sp, 0, 128), IND(A("R"), A(sll, 0, 8))); cp("s", A(sp, 128, 256), IND(A("P"), A(sll, 0, 8)))
         send(A(sll), A("LLa%d" % t), A("LLb%d" % t), "aL%d" % t)
@@ -575,9 +610,7 @@ def rank_program(g, core, T, topo):
         cp("s", A("RF", 0, V), IND(A("R"), A("FL")))
         for kk in range(1, 8):
             if kk in NX_S:
-                s, bank = (512 * kk, 512 * kk + 512), A("pb%d" % (2 + kk % 2))
-                cp("s", A("dx", *s), IND(A("xF"), A("CK%d" % u, 32 * kk, 32 * kk + 32)))
-                mm(bank, A("I"), A("dx", *s), True, False); mm(bank, A("nI"), A("xv2"), False, True)
+                xscalar(u, kk)
             else:
                 xgather(u, kk)
         for kk in range(1, 8):
@@ -585,15 +618,12 @@ def rank_program(g, core, T, topo):
                 act(A("ab", 512 * kk, 512 * kk + 512), A("pb%d" % (2 + kk % 2)), AF.Abs)
             else:
                 xabs(kk)
-        cp("s", A("PF", 0, V), IND(A("P"), A("FL")))
-        dup("s", "Pv2", "P", u); dup("s", "Rv2", "R", u)
+        dup("s", "Rv2", "R", u)
         act(A("SO", t, V, 4), A("sn"), AF.Copy, scale=A("okc"))
-        halves(u, 1)
         keyinit()
         for kk in range(8):
             keymm(kk, "ab", "selD")
-        cp("v", A("Mi"), A("Mf")); ts(A("Mj"), A("Mi"), 31, ALU.bitwise_and); ts(A("Mk"), A("Mj"), 1024.0, ALU.mult)
-        ts(A("thC"), A("thK"), A("Mk"), ALU.add)
+        cupdate()
         if u + 1 < ROUNDS:
             cklist_d(u + 1)
         ll = {d: "LL%s%d" % (d, t) for d in "ab"}

import math
from concourse.bass import DstId, RemoteDMATransfer
from concourse.mybir import AluOpType as ALU, AxisListType, ActivationFunctionType as AF

V, G, W, N, ROUNDS = 1024, 768, 2560, 4, 4
BIGX = 8192.0
HASLIM = 4100.0 * 1024
EQ = 1048576.0
NS_P = ((0, 1, 2, 3, 4, 5, 6, 7),) + ((3, 4, 5, 6, 7),) * 3
NX_S = ()
NV3 = 1

b, f, i4, u2 = "bfloat16", "float32", "int32", "uint16"
_S = {
    "X": (1024, b), "R": (1024, b), "P": (1024, b), "xF": (2560, b), "RF": (2560, b), "PF": (2560, b), "xm": (1024, b),
    "FB": (1280, b), "IB": (1024, b), "ni": (256, i4),
    "ci": (1024, i4), "si": (1024, i4), "CF": (1024, f), "CfE": (1024, f), "CfO": (1024, f), "NHI": (256, b), "NLO": (256, b),
    "SO": (1024, f), "SE": (1024, f), "SL0": (512, u2), "SL1": (512, u2),
    "D1": (512, f), "T1": (512, f), "T2": (496, f), "ckf": (256, f), "CK0": (256, u2), "CK1": (256, u2), "CK2": (256, u2), "CK3": (256, u2),
    "ones": (512, b), "I": (128, b), "nI": (128, b), "bI": (128, b), "U": (128, b), "E0": (128, b), "B16": (128, b),
    "EK": (2048, b), "BL": (2048, b), "SelL": (2048, b), "RH": (2048, b), "kc": (512, b), "rst": (1024, b),
    "SA": (128, b), "SB": (128, b), "SN": (128, b), "rows2": (256, b), "zb": (128, b),
    "selD": (16, b), "selO": (16, b), "selp": (16, b), "seln": (16, b), "sFp": (16, b), "sFn": (16, b), "FS": (16, b), "FH": (16, b), "gm": (16, f),
    "gmi": (16, i4), "mi16": (16, f), "mp": (16, f), "pw": (16, f), "sj": (16, f),
    "pi": (1, i4), "gi": (1, i4), "ii": (1, i4), "ei": (1, i4), "oki": (1, i4), "mI": (128, i4), "mG": (128, i4), "mGf": (128, f),
    "pf": (1, f), "gf": (1, f), "iF": (1, f), "i4c": (1, f), "modd": (1, f), "meven": (1, f), "okc": (1, f), "ekc": (1, f),
    "wcol": (1, f), "il1": (1, f), "wlo": (1, f), "whi": (1, f), "wF": (1, f), "wFn": (1, f), "fhc": (1, f), "c7": (1, f), "c8": (1, f), "mone": (1, f), "c64": (1, f),
    "cb": (2, f), "VL": (128, f), "VR": (96, f), "CC": (96, f), "V0": (96, f), "NG": (96, b), "NG1": (96, b), "kI": (128, b), "chz": (96, b), "thT": (16, f), "thA": (16, f),
    "thr": (8, i4), "thb": (8, i4), "thK": (16, f), "thC": (16, f), "Mf": (1, f), "Mi": (1, i4), "Mj": (1, i4), "Mk": (1, f),
    "xv2": (512, b), "Rv2": (512, b), "Pv2": (512, b), "dx": (4096, b), "ab": (4096, b), "oR": (4096, b), "oP": (4096, b), "pc": (4096, b),
    "ka": (256, f), "t1": (256, f), "wk": (512, f), "wi": (128, i4), "dec": (32, b), "dec2": (48, b), "rowsN": (256, b), "nl": (16, u2),
    "bits": (256, b), "Ae": (256, b), "Ao": (256, b), "Bk": (256, b), "tr": (512, b), "mx": (16, f), "win": (16, b), "rowsW": (512, b),
    "bd": (32, f), "bl": (16, f), "bq": (32, f), "bq2": (32, f), "LL": (32, u2), "bu": (16, u2), "Rn": (256, b), "Pn": (256, b), "xs": (256, f), "xi": (256, i4),
    "sn": (256, f), "FL": (64, u2), "g3": (8192, b), "s3": (8192, b), "oi": (256, f), "dC": (256, f),
    "ch": (96, b), "xw": (768, f), "pos": (96, b), "FpT": (96, f), "dF": (96, f), "Fpb": (96, b), "rowsP": (768, b), "rowsF": (768, b), "pl": (48, u2), "SLB": (896, b),
    "GRa": (896, b), "GRb": (896, b), "GPa": (896, b), "GPb": (896, b),
}
_WHERE, _POOL = {}, {f: 0, i4: 0, u2: 0, b: 0}
SCRATCH = {}
_OWN = ("nl", "pl", "FL", "LL", "bu", "SelL", "SA", "SB", "SN")
for _n, (_c, _d) in _S.items():
    if _c <= 128 and _n not in _OWN:
        _WHERE[_n] = ("pool_" + _d, _POOL[_d]); _POOL[_d] += _c + (-_c) % 16
    else:
        SCRATCH[_n] = ("sbuf", [128, _c], _d); _WHERE[_n] = (_n, 0)
for _d in _POOL:
    if _POOL[_d]:
        SCRATCH["pool_" + _d] = ("sbuf", [128, _POOL[_d]], _d)
for _r in range(3):
    for _n, _c, _d in (("SRP%d", 256, b), ("SLL%d", 56, u2), ("LRa%d", 256, b), ("LRb%d", 256, b), ("LLa%d", 56, u2), ("LLb%d", 56, u2)):
        SCRATCH[_n % _r] = ("sbuf", [128, _c], _d); _WHERE[_n % _r] = (_n % _r, 0)
for _r in range(8):
    SCRATCH["pb%d" % _r] = ("psum", [128, 512], f); _WHERE["pb%d" % _r] = ("pb%d" % _r, 0)
ND = 24
SEMAPHORES = ["qv", "qs", "qt", "qg", "iR", "iP", "loc", "li"] + ["aR%d" % r for r in range(3)] + ["aL%d" % r for r in range(3)] + ["d%d" % k for k in range(ND)]


def rank_program(g, core, T, topo):
    rank = T.rank_of(core)
    if rank is None:
        return
    eng = {"v": g.vector, "s": g.scalar, "t": g.tensor, "g": g, "y": g.sync}
    cnt = {q: 0 for q in eng}; clk = {q: {} for q in eng}; hist = {}; info = []; total = {}; nd = [0]

    def A(n, c0=0, c1=None, st=1, p0=0, p1=128):
        t, o = _WHERE[n]
        if c1 is None:
            c1 = _S[n][0] if n in _S else SCRATCH[n][1][1]
        ap = T[t][p0:p1, o + c0:o + c1] if st == 1 else T[t][p0:p1, o + c0:o + c1:st]
        return (ap, [(n, c0, c1, st)])

    def IND(w, o):
        return (w[0].indirect(o[0]), w[1] + o[1])

    def HB(ap):
        return (ap, [])

    def covers(a0, a1, st, e):
        return a0 <= e[0] and e[1] <= a1 and (st == 1 or (e[4] == st and (e[0] - a0) % st == 0))

    def sync(q, rd, wr, me):
        need = set()
        for regs, isw in ((rd, False), (wr, True)):
            for n, a0, a1, st in regs:
                ps = n[:2] == "pb"
                for e in hist.get(n, ()):
                    over = e[0] < a1 and a0 < e[1] and (e[0] - a0) % math.gcd(st, e[4]) == 0
                    eq = info[e[2]][0]
                    if ps:
                        if eq != q or (over and e[3] and q != "t"):
                            need.add(e[2])
                    elif over and (e[3] or isw):
                        need.add(e[2])
        for o in sorted(need, reverse=True):
            _, sem, val, ck = info[o]
            if clk[q].get(sem, 0) >= val:
                continue
            eng[q].wait_ge(T.sem[sem], val)
            for s, v in list(ck.items()) + [(sem, val)]:
                if clk[q].get(s, 0) < v:
                    clk[q][s] = v
        for regs, isw in ((rd, False), (wr, True)):
            for n, a0, a1, st in regs:
                ps = n[:2] == "pb"
                if ps:
                    h = [e for e in hist.get(n, ()) if info[e[2]][0] == me[1] and not (covers(a0, a1, st, e) and isw == e[3])]
                elif isw:
                    h = [e for e in hist.get(n, ()) if not covers(a0, a1, st, e)]
                else:
                    h = [e for e in hist.get(n, ()) if not (not e[3] and covers(a0, a1, st, e) and info[e[2]][0] == q)]
                h.append((a0, a1, me[0], isw, st)); hist[n] = h

    def op(q, call, rd, wr):
        me = len(info)
        rr = [x for r in rd for x in r[1]]; ww = [x for r in wr for x in r[1]]
        info.append((q, "q" + q, cnt[q] + 1, {}))
        sync(q, rr, ww, (me, q))
        if q == "g" and clk[q].get("qg", 0) < cnt[q]:
            g.wait_ge(T.sem["qg"], cnt[q]); clk[q]["qg"] = cnt[q]
        cnt[q] += 1
        info[me] = (q, "q" + q, cnt[q], dict(clk[q]))
        call(eng[q]).then_inc(T.sem["q" + q], 1); total["q" + q] = cnt[q]

    def dma(q, out, in_):
        me = len(info); s = "d%d" % nd[0]; nd[0] += 1
        info.append(("d" + s, s, 16, {}))
        sync(q, in_[1], out[1], (me, "d" + s))
        info[me] = ("d" + s, s, 16, dict(clk[q])); total[s] = 16
        eng[q].dma_start(out=out[0], in_=in_[0]).then_inc(T.sem[s], 16)

    def arrive(sem, val, regs):
        me = len(info); info.append(("x", sem, val, {})); total[sem] = val
        for r in regs:
            for n, a0, a1, st in r[1]:
                hist.setdefault(n, []).append((a0, a1, me, True, st))

    prev, nxt = T.cores[(rank - 1) % N], T.cores[(rank + 1) % N]
    mk = min(topo.mask(core, prev), topo.mask(core, nxt))
    ne = len([e for e in topo.engines(core, prev) if mk >> e & 1])

    def send(src, to_prev, to_next, sem, loc="loc"):
        sync("g", src[1], [], (len(info), "x")); info.append(("x", loc, 2 * ne, {}))
        ids = []
        for d in (prev, nxt):
            rid, pid, _ = topo.addr(d); ids.append(DstId(rid=rid, pnc=pid))
        g.remote_dma_fused([RemoteDMATransfer(dst_ids=ids, dma_engine_mask=mk, remote_sem=T.sem[sem], srcs=[src[0]], dsts=[to_prev[0], to_next[0]])], local_sem=T.sem[loc])
        total[loc] = total.get(loc, 0) + ne

    def cp(q, out, in_):
        if q == "s":
            op("s", lambda e: e.activation(out=out[0], in_=in_[0], func=AF.Copy), [in_], [out])
        else:
            op("v", lambda e: e.tensor_copy(out=out[0], in_=in_[0]), [in_], [out])

    def tt(out, a, c, o):
        op("v", lambda e: e.tensor_tensor(out=out[0], in0=a[0], in1=c[0], op=o), [a, c], [out])

    def ts(out, a, s1, o1, s2=None, o2=None):
        rd = [a] + [s for s in (s1, s2) if isinstance(s, tuple)]
        v1 = s1[0] if isinstance(s1, tuple) else s1
        v2 = s2[0] if isinstance(s2, tuple) else s2
        if o2 is None:
            op("v", lambda e: e.tensor_scalar(out=out[0], in0=a[0], scalar1=v1, scalar2=None, op0=o1), rd, [out])
        else:
            op("v", lambda e: e.tensor_scalar(out=out[0], in0=a[0], scalar1=v1, scalar2=v2, op0=o1, op1=o2), rd, [out])

    def act(out, in_, fn, bias=None, scale=None, accum=None):
        kw = {}
        rd = [in_]; wr = [out]
        if bias is not None:
            kw["bias"] = bias[0]; rd.append(bias)
        if scale is not None:
            kw["scale"] = scale[0]; rd.append(scale)
        if accum is not None:
            kw["accum_out"] = accum[0]; wr.append(accum)
        op("s", lambda e: e.activation(out=out[0], in_=in_[0], func=fn, **kw), rd, wr)

    def ms(out, c):
        op("v", lambda e: e.memset(out[0], c), [], [out])

    def mm(out, l, r, start, stop):
        op("t", lambda e: e.matmul(out=out[0], lhsT=l[0], rhs=r[0], start=start, stop=stop), [l, r], [out])

    def iota(out, pat, base, cmul, small=False):
        kw = {"allow_small_or_imprecise_dtypes": True} if small else {}
        op("g", lambda e: e.iota(out[0], pat, base, cmul, **kw), [], [out])

    def sel(out, in_, pat, o, fill, base, cmul):
        op("g", lambda e: e.affine_select(out[0], in_[0], pat, o, fill, base, cmul), [in_], [out])

    def rsum(out, in_):
        op("v", lambda e: e.tensor_reduce(out=out[0], in_=in_[0], axis=AxisListType.X, op=ALU.add), [in_], [out])

    def dup(q, out, src, t):
        for h in (0, 256):
            cp(q, A(out, h, h + 256), A(src, t, V, 4))

    def cklist_d(t):
        for e, src in ((0, "CfE"), (1, "CfO")):
            for i in range(16):
                sel(A("D1", 16 * e + i, 512, 32), A(src, 4 * i + t, V, 64), [[0, 16]], ALU.is_equal, 0.0, 0, 0)

    def turn():
        op("v", lambda e: e.transpose(out=A("T1")[0], in_=A("D1")[0]), [A("D1")], [A("T1")])

    def cklist_t():
        turn()
        tt(A("T2"), A("T1", 0, 496), A("T1", 16, 512), ALU.add)
        for k in range(16):
            sel(A("ckf", 16 * k, 16 * k + 16), A("T2", k, 496, 32), [[0, 16]], ALU.is_equal, 0.0, 0, 0)

    def halves(t, which):
        n, o, s = (("NHI", ALU.arith_shift_right, 6), ("NLO", ALU.bitwise_and, 63))[which]
        ts(A("ni"), A("ci", t, V, 4), s, o); cp("v", A(n), A("ni"))

    def xgather(t, kk):
        s = (512 * kk, 512 * kk + 512)
        tt(A("dx", *s), IND(A("xF"), A("CK%d" % t, 32 * kk, 32 * kk + 32)), A("xv2"), ALU.subtract)

    def xscalar(t, kk):
        s, bank = (512 * kk, 512 * kk + 512), A("pb%d" % (2 + kk % 2))
        cp("s", A("dx", *s), IND(A("xF"), A("CK%d" % t, 32 * kk, 32 * kk + 32)))
        mm(bank, A("I"), A("dx", *s), True, False); mm(bank, A("nI"), A("xv2"), False, True)

    def xabs(kk):
        s = (512 * kk, 512 * kk + 512)
        act(A("ab", *s), A("dx", *s), AF.Abs)

    def keyinit():
        for half in (0, 1):
            o = A("pb%d" % half, 0, 256)
            mm(o, A("E0"), A("kc", 256 * half, 256 * half + 256), True, False)
            for hv in range(4):
                h, var = hv // 2, hv % 2
                mm(o, A(("NHI", "NLO")[var], 128 * h, 128 * h + 128), A("RH", 512 * hv + 256 * half, 512 * hv + 256 * half + 256), False, False)

    def keymm(kk, buf, w, last=False):
        bank = "pb%d" % (kk // 4)
        for k in (2 * kk, 2 * kk + 1):
            for h in (0, 1):
                o = 32 * (k % 8) + h
                mm(A(bank, o, o + 32 - h, 2), A(buf, 256 * k + 128 * h, 256 * k + 128 * h + 128), A(w), False, last and k % 8 == 7 and h == 1)

    def bits2list(out, src, n):
        for i in range(16):
            mm(out, A("BL", 128 * i, 128 * i + 128), A(src, i, n, 16), i == 0, i == 15)

    def rows2list(out, src, n, kp):
        for i in range(16):
            mm(out, A("SelL", 128 * i, 128 * i + 128, p1=kp), A(src, i, n, 16, p1=kp), i == 0, i == 15)

    def chsum(buf, w, cs=range(6), stop=False):
        for c in cs:
            mm(A("pb4", 16 * c, 16 * c + 16), A(buf, 128 * c, 128 * c + 128), A(w), False, stop and c == 5)

    def ftsum(col, w):
        for c in range(6):
            mm(A("pb6", col + 16 * c, col + 16 * c + 16), A("FB", 128 * c, 128 * c + 128), A(w), True, True)

    dma("s", A("R", 0, G), HB(T.reach[:, 0:G])); dma("y", A("ci"), HB(T.cand[:]))
    dma("s", A("P", 0, G), HB(T.past[:, 0:G])); dma("y", A("X"), HB(T.x[:]))
    dma("s", A("R", G, V), HB(T.reach[:, G:V])); dma("y", A("thr", p1=1), HB(T.th[:]))
    dma("s", A("P", G, V), HB(T.past[:, G:V])); dma("y", A("si"), HB(T.succ[:]))
    dma("y", A("RF", 0, V), HB(T.reach[:])); dma("y", A("PF", 0, V), HB(T.past[:]))

    iota(A("pi"), [[0, 1]], 0, 1)
    ms(A("ones"), 1.0)
    iota(A("gmi"), [[0, 2], [1, 8]], 0, 0)
    iota(A("mi16"), [[1, 16]], 0, 0, True)
    iota(A("mI"), [[1, 128]], 0, 0)
    iota(A("VL", 0, 16), [[64, 16]], 0, 0, True); iota(A("VL", 16, 32), [[16, 16]], 1024, 0, True)
    send(A("R", 0, G), A("RF", V, V + G), A("RF", V + G, W), "iR", "li")
    send(A("P", 0, G), A("PF", V, V + G), A("PF", V + G, W), "iP", "li")
    arrive("iR", 2 * ne, [A("RF", V, W)]); arrive("iP", 2 * ne, [A("PF", V, W)])
    sel(A("xF", 0, V), A("X"), [[0, 256], [1, 4]], ALU.not_equal, BIGX, 0, 0)
    ts(A("gi"), A("pi"), 4, ALU.arith_shift_right); ts(A("ii"), A("pi"), 15, ALU.bitwise_and)
    ts(A("ei"), A("gi"), 1, ALU.bitwise_and)
    cp("v", A("modd"), A("ei")); cp("v", A("iF"), A("ii")); cp("v", A("gf"), A("gi")); cp("v", A("gm"), A("gmi"))
    ts(A("meven"), A("modd"), -1.0, ALU.mult, 1.0, ALU.add)
    ts(A("gm"), A("gm"), A("gf"), ALU.is_equal)
    ts(A("selD"), A("gm"), 1024.0, ALU.mult); ts(A("selO"), A("gm"), 8388608.0, ALU.mult)
    ms(A("xF", V, W), BIGX)
    ms(A("cb", 0, 1), -10.0 * EQ); ms(A("cb", 1, 2), 1.0)
    ts(A("mi16"), A("mi16"), A("iF"), ALU.is_equal)
    ts(A("sj"), A("mi16"), -2.0, ALU.mult, 1.0, ALU.add)
    ts(A("c64"), A("iF"), 8.0, ALU.is_lt, 63.0, ALU.mult); ts(A("c64"), A("c64"), 1.0, ALU.add)
    ts(A("il1"), A("iF"), 10.0, ALU.is_lt)
    ts(A("IB", 0, 1), A("il1"), -1.0, ALU.mult)
    ms(A("EK"), 0.0)
    ts(A("mG"), A("mI"), 4, ALU.arith_shift_right); cp("v", A("mGf"), A("mG")); ts(A("B16"), A("mGf"), A("gf"), ALU.is_equal)
    ts(A("CfE", 0, 256), A("ci", 0, V, 4), A("meven"), ALU.mult)
    ts(A("CfO", 0, 256), A("ci", 0, V, 4), A("modd"), ALU.mult)
    for i in range(16):
        cp("s" if i < 11 else "v", A("D1", i, 512, 32), A("CfE", i, 256, 16))
    for i in range(16):
        cp("v", A("D1", 16 + i, 512, 32), A("CfO", i, 256, 16))
    turn()
    dup("s", "xv2", "X", 0)
    for k in range(16):
        cp("s", A("EK", 128 * k + k, 128 * k + 128, 16), A("B16", k, 128, 16))
    for j in range(10):
        act(A("IB", 2 ** j, 2 ** (j + 1)), A("IB", 0, 2 ** j), AF.Copy, scale=A("sj", j, j + 1))
    for k in range(16):
        tt(A("ckf", 16 * k, 16 * k + 16), A("T1", k, 512, 32), A("T1", 16 + k, 512, 32), ALU.add)
    cp("v", A("CK0"), A("ckf"))
    for kk in range(7):
        xgather(0, kk)
    halves(0, 0); halves(0, 1)
    dma("y", A("SelL", p1=8), (T.EK[0:128:16, :], A("EK")[1])); dma("y", A("SelL", p0=8, p1=16), (T.EK[0:128:16, :], A("EK")[1]))
    ms(A("rows2"), 0.0)
    sel(A("E0"), A("ones", 0, 128), [[0, 128]], ALU.is_equal, 0.0, 0, 1)
    iota(A("kc"), [[64, 16], [0, 32]], 0, 0, True)
    for hv in range(4):
        sel(A("RH", 512 * hv, 512 * hv + 512), A("ones"), [[-1, 16], [-16, 16], [4096, 2]], ALU.is_equal, 0.0, 128 * (hv % 2) - 4096 * (hv // 2), 1)
    sel(A("I"), A("ones", 0, 128), [[-1, 128]], ALU.is_equal, 0.0, 0, 1)
    sel(A("nI"), A("I"), [[-1, 128]], ALU.not_equal, -1.0, 0, 1)
    xscalar(0, 7)
    for kk in range(7):
        xabs(kk)
    act(A("ab", 3584, 4096), A("pb3"), AF.Abs)
    iota(A("SN", p1=65), [[0, 128]], 0, 0, True)
    sel(A("SN", p1=65), A("SN", p1=65), [[1, 8], [0, 16]], ALU.not_equal, -32768.0, 16, -1)
    iota(A("rows2", p0=32, p1=33), [[1, 256]], 0, 0, True)
    op("g", lambda e: e.partition_broadcast(A("thb")[0], A("thr", p1=1)[0], 128), [A("thr")], [A("thb")])
    iota(A("VR"), [[0, 6], [1, 2], [0, 8]], 0, 0, True); iota(A("CC"), [[128, 6], [0, 16]], 128, 0, True)
    keyinit()
    for kk in range(8):
        keymm(kk, "ab", "selD")

    def later():
        cp("v", A("CF"), A("ci"))
        ms(A("pw"), 0.0)
        for i in range(10):
            ms(A("pw", i, i + 1), 2.0 ** (i - 1))
        tt(A("mp"), A("mi16"), A("pw"), ALU.mult); rsum(A("wcol"), A("mp"))
        ms(A("zb"), 0.0)
        ms(A("rows2", p0=64, p1=65), 1.0)
        for n in ("SA", "SB"):
            ms(A(n, p1=65), 0.0)
        ms(A("rst"), 0.0)
        for n, r, i, w in (("SA", 32, 12, 1.0), ("SA", 64, 13, 1.0), ("SA", 64, 14, 1.0), ("SA", 64, 15, 1.0), ("SB", 64, 10, 4096.0), ("SB", 64, 11, 256.0), ("SB", 64, 12, 1.0), ("SB", 32, 15, -1.0)):
            ms(A(n, i, 128, 16, p0=r, p1=r + 1), w)
        for n, c, i, w in (("SA", 0, 10, 1.0), ("SA", 8, 11, 1.0), ("SB", 0, 13, -4096.0), ("SB", 8, 14, -256.0)):
            ts(A(n, i, 128, 16, p1=16), A("I", c, c + 8, p1=16), w, ALU.mult)
        ms(A("rst", 0, 1024, 16), 1000.0)
        ms(A("thT"), 1.0); ms(A("thT", 0, 16, 2), 10.0 * EQ + 1.0)
        sel(A("U"), A("ones", 0, 128), [[1, 128]], ALU.is_ge, 0.0, 0, -1)
        dma("y", A("FB", 0, V), A("IB"))
        ts(A("bI"), A("I"), EQ, ALU.mult)
        ts(A("oki"), A("ii"), 1, ALU.bitwise_and); cp("v", A("okc"), A("oki")); ts(A("ekc"), A("okc"), -1.0, ALU.mult, 1.0, ALU.add)
        for h in (0, 1):
            ts(A("thK", h, 16, 2), A("thb"), 1024.0, ALU.mult)
        cp("v", A("thC"), A("thK"))
        ts(A("i4c"), A("iF"), 4.0, ALU.mult)
        ts(A("VL", 16, 32), A("VL", 16, 32), A("iF"), ALU.add)
        for t in (1, 2, 3):
            ts(A("VL", 32 * t, 32 * t + 16), A("VL", 0, 16), A("i4c"), ALU.add, float(t), ALU.add)
            cp("v", A("VL", 32 * t + 16, 32 * t + 32), A("VL", 16, 32))
        ts(A("VL", 0, 16), A("VL", 0, 16), A("i4c"), ALU.add)
        cp("v", A("SO"), A("si"))

    def later1():
        act(A("SE"), A("SO"), AF.Copy, scale=A("ekc"))
        act(A("SO"), A("SO"), AF.Copy, scale=A("okc"))
        cp("v", A("SL0"), A("si", 0, V, 2))
        cp("s", A("SLB", 0, 128), A("IB", G, G + 128))

    def later2():
        cp("v", A("SL1"), A("si", 1, V, 2))
        cp("v", A("pf"), A("pi"))
        ts(A("c7"), A("iF"), 7.0, ALU.is_lt); tt(A("wlo"), A("c7"), A("wcol"), ALU.mult); tt(A("whi"), A("wcol"), A("wlo"), ALU.subtract)
        ts(A("c8"), A("iF"), 8.0, ALU.is_ge); tt(A("fhc"), A("c8"), A("il1"), ALU.mult)
        ts(A("wF"), A("wcol"), 16384.0, ALU.mult); ts(A("wFn"), A("wcol"), -16384.0, ALU.mult)
        ms(A("mone"), -1.0)
        cp("s", A("selp"), A("gm"))
        for o, w in (("seln", "mone"), ("sFp", "wF"), ("sFn", "wFn"), ("FH", "fhc")):
            act(A(o), A("gm"), AF.Copy, scale=A(w))
        act(A("FS", 0, 8), A("gm", 0, 8), AF.Copy, scale=A("wlo")); act(A("FS", 8, 16), A("gm", 8, 16), AF.Copy, scale=A("whi"))
        ts(A("V0"), A("VR"), -1.0, ALU.mult, 1.0, ALU.add)
        tt(A("CC"), A("VR"), A("CC"), ALU.mult); ts(A("VR"), A("V0"), A("pf"), ALU.mult); tt(A("NG"), A("CC"), A("VR"), ALU.add); tt(A("NG1"), A("NG"), A("V0"), ALU.add)
        ts(A("kI"), A("I"), -1024.0, ALU.mult)
        ftsum(0, "FS"); cp("v", A("FpT"), A("pb6", 0, 96))
        for s, d in (("RF", "GR"), ("PF", "GP")):
            dma("y", A(d + "a", 0, G), A(s, V, V + G)); dma("y", A(d + "b", 0, G), A(s, V + G, W))

    for t in range(ROUNDS):
        last = t == ROUNDS - 1
        ckt = "CK%d" % t; u = t + 1
        if t == 0:
            dup("s", "Pv2", "P", t); dup("s", "Rv2", "R", t)
        nsp = NS_P[t]; first = [True]

        def vchunk(n, kk):
            s = (512 * kk, 512 * kk + 512); off = A(ckt, 32 * kk, 32 * kk + 32)
            if n == "oR":
                tt(A("oR", *s), IND(A("RF"), off), A("Pv2"), ALU.is_le)
            else:
                tt(A("oP", *s), IND(A("PF"), off), A("Rv2"), ALU.is_ge)

        def pgather(kk):
            s = (512 * kk, 512 * kk + 512)
            cp("s", A("pc", *s), IND(A("PF"), A(ckt, 32 * kk, 32 * kk + 32)))
            bank = A("pb%d" % (2 + kk % 2))
            mm(bank, A("I"), A("pc", *s), True, False); mm(bank, A("nI"), A("Rv2"), False, True)

        def prelu(kk):
            act(A("oP", 512 * kk, 512 * kk + 512), A("pb%d" % (2 + kk % 2)), AF.Relu, bias=A("cb", 1, 2))

        def olist(kk):
            for k in (2 * kk, 2 * kk + 1):
                for n in ("oR", "oP"):
                    mm(A("pb7", 0, 256), A("EK", 128 * k, 128 * k + 128), A(n, 256 * k, 256 * k + 256), first[0], False)
                    first[0] = False
        work = [(n, kk) for kk in range(8) for n in ("oR", "oP") if n == "oR" or kk not in nsp]
        ev = [(i + 1.0, 0, n, kk) for i, (n, kk) in enumerate(work)]
        ev += [(1.7 * j + 1.0, 1, "g", kk) for j, kk in enumerate(nsp)] + [(1.7 * j + 2.8, 2, "r", kk) for j, kk in enumerate(nsp)]
        left = {0: 16, 1: 16}
        for _, _, n, kk in sorted(ev):
            if n == "g":
                pgather(kk)
                continue
            if n == "r":
                prelu(kk)
            else:
                vchunk(n, kk)
            n = "oP" if n == "r" else n
            left[kk // 4] -= 2
            keymm(kk, n, "selO", left[kk // 4] == 0)
        if t == 0:
            later()
            act(A("CfE"), A("CF"), AF.Copy, scale=A("meven")); act(A("CfO"), A("CF"), AF.Copy, scale=A("modd"))
            act(A("BL"), A("EK"), AF.Copy, scale=A("wcol"))
            cklist_d(1)
        if not last:
            halves(u, 0); halves(u, 1)
        cp("s", A("ka"), A("pb0", 0, 256))
        tt(A("t1"), A("pb1", 0, 256), A("ka"), ALU.min)
        tt(A("wk", 0, 128), A("t1", 0, 128), A("t1", 128, 256), ALU.min)
        tt(A("wk", 128, 192), A("wk", 0, 64), A("wk", 64, 128), ALU.min)
        tt(A("wk", 192, 224), A("wk", 128, 160), A("wk", 160, 192), ALU.min)
        m0 = A("wk", 192, 208)
        ts(A("wi", 0, 32), A("wk", 192, 224), 16777215.0, ALU.min)
        ts(A("wk", 224, 256), A("wk", 192, 224), HASLIM, ALU.is_lt)
        ts(A("wi", 32, 64), A("wi", 0, 32), 63, ALU.bitwise_and)
        tt(A("dec"), A("wi", 32, 64), A("wk", 224, 256), ALU.mult)
        for h in (0, 1):
            mm(A("pb5", 128 * h, 128 * h + 128, p1=16), A("dec", h, 32, 2), A("I"), True, True)
        act(A("rowsN", p1=16), A("pb5", 0, 256, p1=16), AF.Copy, scale=A("c64", p1=16))
        rows2list(A("pb6", 0, 16), "rowsN", 256, 16)
        tt(A("wk", 272, 288), m0, A("thC"), ALU.is_ge)
        ts(A("wk", 304, 320), m0, 4095.0 * 1024, ALU.min)
        ts(A("wk", 288, 304), A("wk", 272, 288), 4095.0 * 1024, ALU.mult)
        ts(A("dec2", 32, 48), m0, HASLIM, ALU.is_ge)
        tt(A("wi", 64, 80), A("wk", 288, 304), A("wk", 304, 320), ALU.max)
        ts(A("wi", 80, 96), A("wi", 64, 80), 14, ALU.arith_shift_right)
        ts(A("wi", 112, 128), A("wi", 64, 80), 10, ALU.arith_shift_right)
        ts(A("wi", 96, 112), A("wi", 112, 128), 15, ALU.bitwise_and)
        cp("v", A("dec2", 0, 32), A("wi", 80, 112))
        for h in (0, 1):
            mm(A("pb2", 128 * h, 128 * h + 128, p1=24), A("dec2", h, 48, 2), A("I"), True, True)
        cp("s", A("rows2", p1=24), A("pb2", 0, 256, p1=24))
        cp("v", A("nl"), A("pb6", 0, 16))
        cp("v", A("bits"), IND(A("FB", 0, V), A("nl")))
        tt(A("wk", 320, 336), A("wk", 272, 288), A("thT"), ALU.mult)
        tt(A("thA"), A("thT"), A("wk", 320, 336), ALU.subtract); ts(A("thA"), A("thA"), 1.0, ALU.subtract)
        mm(A("pb5", 0, 256), A("SA", p1=65), A("rows2", p1=65), True, False); mm(A("pb6", 0, 256), A("SB", p1=65), A("rows2", p1=65), True, False)
        mm(A("pb5", 0, 256), A("I"), A("bits"), False, True); mm(A("pb6", 0, 256), A("bI"), A("bits"), False, True)
        ts(A("Ae"), A("pb5", 0, 256), A("meven"), ALU.mult)
        cp("s", A("Bk"), A("pb6", 0, 256))
        ts(A("Ao"), A("pb5", 0, 256), A("modd"), ALU.mult)
        for gp in range(4):
            for e in (0, 1):
                for h in (0, 1):
                    mm(A("pb%d" % (2 * h + gp % 2), 256 * e, 256 * e + 256), A(("Ae", "Ao")[e], 128 * h, 128 * h + 128, p0=32 * gp, p1=32 * gp + 32), A("Bk", p0=32 * gp, p1=32 * gp + 32), True, True)
            for e in (0, 1):
                gg = 2 * gp + e
                bk = A("pb%d" % (gp % 2), 256 * e, 256 * e + 256)
                op("v", lambda q, bk=bk, gg=gg: q.tensor_reduce(out=A("mx", 2 * gg, 2 * gg + 1)[0], in_=bk[0], axis=AxisListType.X, op=ALU.max), [bk], [A("mx", 2 * gg, 2 * gg + 1)])
                act(A("tr", 256 * e, 256 * e + 256), A("pb%d" % (2 + gp % 2), 256 * e, 256 * e + 256), AF.Relu, bias=A("cb", 0, 1), accum=A("mx", 2 * gg + 1, 2 * gg + 2))
        bits2list(A("pb5", 0, 16), "bits", 256)
        tt(A("win"), A("mx"), A("thA"), ALU.is_le)
        ts(A("bl"), A("pb5", 0, 16), 511.5, ALU.add)
        for d, bank in ((0, "pb5"), (256, "pb0")):
            for h in (0, 1):
                mm(A(bank, 128 * h, 128 * h + 128, p1=8), A("win", h, 16, 2), A("I"), True, True)
        tt(A("bd", 0, 16), A("bl"), A("VL", 32 * t, 32 * t + 16), ALU.subtract); tt(A("bd", 16, 32), A("bl"), A("VL", 32 * t + 16, 32 * t + 32), ALU.subtract)
        cp("s", A("rowsW", 0, 256, p1=8), A("pb5", 0, 256, p1=8)); cp("v", A("rowsW", 256, 512, p1=8), A("pb0", 0, 256, p1=8))
        rows2list(A("pb6", 0, 32), "rowsW", 512, 8)
        if t == 0:
            later1()
        cp("v", A("bu"), A("bl"))
        tt(A("dC"), IND(A("CF"), A("bu")), A("ci", t, V, 4), ALU.subtract)
        tt(A("bq"), A("pb6", 0, 32), A("bd"), ALU.mult)
        tt(A("bq2"), A("bq"), A("VL", 32 * t, 32 * t + 32), ALU.add)
        cp("v", A("LL"), A("bq2"))
        be, bt = A("LL", 0, 16), A("LL", 16, 32)
        if not last:
            if t == 0:
                later2()
            mm(A("pb4", 0, 96), A("zb"), A("rst", 0, 96), True, False)
            chsum("R", "selp"); chsum("P", "seln"); chsum("FB", "sFn")
        cp("v", IND(A("FB"), bt), A("IB", t, V, 4))
        bits2list(A("pb5", 0, 64), "FB", V)
        tt(A("Rn"), IND(A("R"), be), A("Rv2", 0, 256), ALU.min)
        cp("s", A("R", t, V, 4), A("Rn"))
        tt(A("sn"), IND(A("SO"), be), A("SE", t, V, 4), ALU.add)
        cp("v", A("SL%d" % (t % 2), t // 2, 512, 2), A("sn"))
        ts(A("FL"), A("pb5", 0, 64), 511.5, ALU.add)
        cp("v", A("RF", 0, 512), IND(A("R"), A("FL", 0, 32))); cp("s", A("RF", 512, V), IND(A("R"), A("FL", 32, 64)))
        par = t % 2

        def g3(q, c):
            cp(q, A("g3", 1024 * c, 1024 * c + 1024), IND(A("RF"), A("SL%d" % par, 64 * c, 64 * c + 64)))

        def s3(c):
            s = (1024 * c, 1024 * c + 1024)
            op("v", lambda e: e.tensor_tensor_scan(out=A("s3", *s)[0], data0=A("rst")[0], data1=A("g3", *s)[0], initial=0.0, op0=ALU.max, op1=ALU.min), [A("rst"), A("g3", *s)], [A("s3", *s)])
        tt(A("xs"), IND(A("X"), be), A("xv2", 0, 256), ALU.add)
        if not last:
            tt(A("Pn"), IND(A("P"), be), A("Pv2", 0, 256), ALU.max)
        for c in range(NV3, 8):
            g3("s", c)
            if c == NV3 and not last:
                cp("s", A("P", t, V, 4), A("Pn"))
        ts(A("xi"), A("xs"), -0.5, ALU.add, 0.5, ALU.mult)
        cp("v", A("X", t, V, 4), A("xi"))
        if last:
            dma("y", HB(T.yx[:]), A("X"))
        else:
            sel(A("xm"), A("X"), [[0, 256], [1, 4]], ALU.not_equal, BIGX, -u, 0)
        for c in range(NV3):
            g3("v", c)
        if not last:
            mm(A("pb6", 192, 208), A("ones", 0, 128), A("win"), True, True)
            ftsum(0, "FS"); ftsum(96, "FH")
            chsum("FB", "sFp"); chsum("P", "selp")
            rsum(A("Mf"), A("pb6", 192, 208))
            ts(A("xw", 0, 96), A("pb6", 96, 192), 1.0, ALU.is_lt)
            tt(A("dF"), A("pb6", 0, 96), A("FpT"), ALU.subtract)
            tt(A("dF"), A("dF"), A("xw", 0, 96), ALU.mult)
            cklist_t()
        for kk in range(8):
            olist(kk)
        mm(A("pb7", 0, 256), A("SN", p1=65), A("rows2", p1=65), False, True)

        def cupdate():
            tt(A("oi"), A("oi"), A("dC"), ALU.mult)
            tt(A("CF", t, V, 4), A("oi"), A("CF", t, V, 4), ALU.add)
        for c0, c1 in ((0, 5), (5, 8)):
            for c in range(c0, c1):
                s3(c)
            if c0 == 0 and last:
                ts(A("oi"), A("pb7", 0, 256), 0.0, ALU.is_gt); cupdate()
                dma("y", HB(T.yc[:]), A("CF"))
            o = A("R", par + 128 * c0, 128 * c1, 2)
            tt(o, A("s3", 1024 * c0 + 15, 1024 * c1, 16), o, ALU.min)
            if not last:
                chsum("R", "seln", range(c0, min(c1, 6)), c1 == 8)
            else:
                dma("sy"[c0 // 5], HB(T.yr[:, 128 * c0:128 * c1]), A("R", 128 * c0, 128 * c1))
        if last:
            break
        cp("s", A("xF", 0, V), IND(A("xm"), A("FL")))
        dup("s", "xv2", "X", u); dup("s", "Pv2", "P", u)
        ts(A("ch"), A("pb4", 0, 96), 0.0, ALU.not_equal)
        mm(A("pb5", 0, 96), A("U"), A("ch"), True, False)
        for s in range(1, 6):
            mm(A("pb5", 16 * s, 96), A("ones", 0, 128), A("ch", 0, 96 - 16 * s), False, False)
        mm(A("pb5", 0, 96), A("kI"), A("ch"), False, True)
        tt(A("chz"), A("ch"), A("V0"), ALU.mult)
        mm(A("pb6", 0, 96), A("nI"), A("NG1"), True, False)
        mm(A("pb6", 0, 96), A("U"), A("chz"), False, False)
        for s in range(1, 6):
            mm(A("pb6", 16 * s, 96), A("ones", 0, 128), A("chz", 0, 96 - 16 * s), False, s == 5)
        cp("v", A("Mi"), A("Mf")); ts(A("Mj"), A("Mi"), 31, ALU.bitwise_and)
        ts(A("xw", 96, 192), A("pb5", 0, 96), 128.0 - 1024.0, ALU.is_le)
        tt(A("pos"), A("pb6", 0, 96), A("xw", 96, 192), ALU.mult)

        def torows(src, rows, b0, b1, q, more=None):
            for c in range(6):
                bank, o = ((b0, 128 * c) if c < 4 else (b1, 128 * c - 512))
                mm(A(bank, o, o + 128, p1=16), A(src, 16 * c, 16 * c + 16), A("I"), True, more is None)
                if more is not None:
                    mm(A(bank, o, o + 128, p1=16), A(more, 16 * c, 16 * c + 16), A("I"), False, True)
            cp("s", A(rows, 0, 512, p1=16), A(b0, 0, 512, p1=16)); cp(q, A(rows, 512, G, p1=16), A(b1, 0, 256, p1=16))
        tt(A("xw", 480, 576), A("dF"), A("xw", 96, 192), ALU.mult)
        torows("pos", "rowsP", "pb5", "pb6", "v", "NG")
        ts(A("oi"), A("pb7", 0, 256), 0.0, ALU.is_gt)
        rows2list(A("pb7", 0, 48), "rowsP", G, 16)
        cp("v", A("CK%d" % u), A("ckf"))
        tt(A("FpT"), A("FpT"), A("xw", 480, 576), ALU.add)
        cp("v", A("Fpb"), A("FpT"))
        xgather(u, 0)
        cp("v", A("pl"), A("pb7", 0, 48))
        torows("Fpb", "rowsF", "pb2", "pb3", "s")
        rows2list(A("pb5", 0, 48), "rowsF", G, 16)
        cp("v", IND(A("SLB"), A("pl")), A("IB", 0, G))
        bits2list(A("pb7", 0, 8), "SLB", 128)
        sp, sll = "SRP%d" % t, "SLL%d" % t
        ts(A(sll, 8, 56), A("pb5", 0, 48), 511.5, ALU.add)
        xabs(0)
        cp("s", A("PF", 0, V), IND(A("P"), A("FL")))
        ts(A("Mk"), A("Mj"), 1024.0, ALU.mult); ts(A("thC"), A("thK"), A("Mk"), ALU.add)
        ts(A(sll, 0, 8), A("pb7", 0, 8), 511.5, ALU.add)
        cp("v", A(sp, 0, 128), IND(A("R"), A(sll, 0, 8))); cp("s", A(sp, 128, 256), IND(A("P"), A(sll, 0, 8)))
        send(A(sll), A("LLa%d" % t), A("LLb%d" % t), "aL%d" % t)
        send(A(sp), A("LRa%d" % t), A("LRb%d" % t), "aR%d" % t)
        arrive("aR%d" % t, 2 * ne, [A("LRa%d" % t), A("LRb%d" % t)]); arrive("aL%d" % t, 2 * ne, [A("LLa%d" % t), A("LLb%d" % t)])
        cp("s", A("SLB", 0, 128), A("IB", G, G + 128))
        cp("s", A("RF", 0, V), IND(A("R"), A("FL")))
        for kk in range(1, 8):
            if kk in NX_S:
                xscalar(u, kk)
            else:
                xgather(u, kk)
        for kk in range(1, 8):
            if kk in NX_S:
                act(A("ab", 512 * kk, 512 * kk + 512), A("pb%d" % (2 + kk % 2)), AF.Abs)
            else:
                xabs(kk)
        dup("s", "Rv2", "R", u)
        act(A("SO", t, V, 4), A("sn"), AF.Copy, scale=A("okc"))
        keyinit()
        for kk in range(8):
            keymm(kk, "ab", "selD")
        cupdate()
        if u + 1 < ROUNDS:
            cklist_d(u + 1)
        ll = {d: "LL%s%d" % (d, t) for d in "ab"}
        for k, tb in ((1, "GP"), (0, "GR")):
            for d in "ab":
                cp("v", IND(A(tb + d), A(ll[d], 0, 8)), A("LR%s%d" % (d, t), 128 * k, 128 * k + 128))
        for k, d in enumerate("ab"):
            cp("s", A("PF", V + G * k, V + G * k + G), IND(A("GP" + d), A(ll[d], 8, 56)))
        cp("v", A("RF", V, V + G), IND(A("GRa"), A(ll["a"], 8, 56)))
        cp("v", A("RF", V + G, V + G + 384), IND(A("GRb"), A(ll["b"], 8, 32)))
        cp("s", A("RF", V + G + 384, W), IND(A("GRb"), A(ll["b"], 32, 56)))

    for s, v in total.items():
        g.wait_ge(T.sem[s], v)
